import numpy as np, ml_dtypes
CORES = [8,136,40,168]
N = 4
BF = ml_dtypes.bfloat16
W, M, TV, S, B = 2048, 192, 6, 1, 8
QN = W // 16
def parts(rng):
    X = rng.integers(0, 256, (N, 8, 16, W)); z = rng.integers(0, 256, (N, 8, 16, M))
    o = np.argsort(rng.random((8, W)), axis=1); A, H, Q = o[:, :8], o[:, 8:40], o[:, 40:40 + QN]; gi = np.arange(8)[None, :, None, None]
    e = rng.integers(0, W, (N, 8, 16, W)); l = rng.integers(0, W, (N, 8, 16, M))
    e = np.where(rng.random(e.shape) < 0.2, H[gi, rng.integers(0, 32, e.shape)], e)
    l[:, :, 0] = H[gi[..., 0], rng.integers(0, 32, (N, 8, M))]
    for q in range(N):
        for g in range(8):
            lanes = rng.permutation(16)[:8]; sub = e[q, g]; sub[lanes[:, None], Q[g][None, :]] = A[g][:, None]
    barred = rng.random((N, 8, M)) < 0.06; barred[:, :, 5] = True
    lb = Q[gi, rng.integers(0, QN, (N, 8, 16, M))]; lb[:, :, 0] = A[gi[..., 0], rng.integers(0, 8, (N, 8, M))]
    keep = (rng.random((N, 8, 1, M)) < 0.5) & (np.arange(16)[None, None, :, None] == rng.integers(1, 16, (N, 8, 1, M)))
    l = np.where(barred[:, :, None, :] & ~keep, lb, l)
    return X, e, l, z, rng.integers(800, 1501, (N, 8))
def pack(X, e, l, z, th):
    return {"xt": np.ascontiguousarray(X.reshape(N, 128, W)).astype(np.float32).astype(BF), "ex": np.ascontiguousarray(e.reshape(N, 128, W)).astype(np.int32),
            "l0": np.ascontiguousarray(l.reshape(N, 128, M)).astype(np.int32), "z0": np.ascontiguousarray(z.reshape(N, 128, M)).astype(np.float32).astype(BF),
            "th": np.ascontiguousarray(th.reshape(N, 8, 1)).astype(np.int32)}
def setup_inputs(rng):
    return pack(*parts(rng))
def setup_inputs_spread(rng):
    def skew(top, rows, n):
        return np.minimum((top * rng.random((N, 8, rows, n)) ** np.exp2(rng.integers(-3, 4, (N, 8, 1, n)))).astype(np.int64), top - 1)
    return pack(skew(256, 16, W), skew(W, 16, W), skew(W, 16, M), skew(256, 16, M), rng.integers(0, 4081, (N, 8)))
def setup_inputs_ends(rng):
    ends = np.array([0, W - 1])
    def bits(n):
        u = rng.random((N, 8, 1, n)); return np.where(u < 0.3, 0, np.where(u < 0.6, 255, 255 * rng.integers(0, 2, (N, 8, 16, n))))
    X = bits(W); z = bits(M); sw = (np.arange(N)[:, None, None] + np.arange(8)[None, :, None]) % 2
    X[..., 0] = 255 * sw; X[..., W - 1] = 255 * (1 - sw); z[..., M - 1] = 0; z[..., 0] = 255
    u = rng.random((N, 8, 1, W)); u[..., 0] *= 0.7; u[..., W - 1] *= 0.7
    e = np.where(u < 0.25, 0, np.where(u < 0.5, W - 1, np.where(u < 0.7, ends[rng.integers(0, 2, (N, 8, 16, W))], rng.integers(0, W, (N, 8, 16, W)))))
    l = np.where(rng.random((N, 8, 16, M)) < 0.7, ends[rng.integers(0, 2, (N, 8, 16, M))], rng.integers(0, W, (N, 8, 16, M)))
    l[:, :, [2, 7, 15], M - 1] = W - 1; l[:, :, 0, M - 1] = 0
    th = np.stack([rng.permutation(np.array([0, 4080] * 4)) for q in range(N)]); th[N - 1] = np.array([0, 4080] * 4)
    return pack(X, e, l, z, th)
def setup_inputs_corners(rng):
    X, e, l, z, th = parts(rng); v = [int(a) for a in rng.permutation(8)]; i = np.arange(M); c = np.arange(W)
    e[:, v[0]] = np.where(rng.random((N, 16, W)) < 0.5, c, e[:, v[0]])
    l[:, v[0]] = np.where(rng.random((N, 16, M)) < 0.4, l[:, v[0], :1], l[:, v[0]]); l[:, v[0], :, ::8] = l[:, v[0], :1, ::8].copy()
    th[:, v[0]] = 4080
    o = rng.permutation(W); A, full, free = o[:8], o[8:8 + W // 2], o[8 + W // 2:]
    for g in (v[1], v[2]):
        e[:, g] = rng.choice(free, (N, 16, W))
        for q in range(N):
            lanes = rng.permutation(16)[:8]; sub = e[q, g]; sub[lanes[:, None], full[None, :]] = A[:, None]
        l[:, g] = rng.choice(full, (N, 16, M)); l[:, g, 0] = rng.choice(A, (N, M))
    l[:, v[2], 1 + i % 15, i] = rng.choice(free, (N, M)); j = i[1::2]
    l[:, v[2], 1 + (j + 7) % 15, j] = rng.choice(free, (N, len(j)))
    th[:, v[1]] = rng.choice(np.array([1, 4079]), N)
    l[:, v[3], 1:] = rng.integers(0, W, (N, 1, M)); th[:, v[3]] = 0
    X[:, v[4]] = X[:, v[4], :, :4].copy()[:, :, rng.integers(0, 4, W)]
    tips = np.array([0, 1, W - 2, W - 1]); e[:, v[5]] = rng.choice(tips, (N, 16, W)); l[:, v[5]] = rng.choice(tips, (N, 16, M))
    l[:, v[6], 1:] = rng.choice(o[-3:], (N, 15, M)); th[:, v[6]] = 4080
    e[:, v[7]] = (c[None, :] + 1 + np.arange(16)[:, None]) % W; l[:, v[7]] = rng.integers(W - 20, W, (N, 16, M))
    return pack(X, e, l, z, th)
def setup_inputs_crowd(rng):
    X, e, l, z, th = parts(rng); X = np.minimum(np.maximum(X, 1), 254)
    sizes = rng.permutation(np.array([1, 2, 3, 16, 64, 256, W, W]))
    for g in range(8):
        pool = rng.permutation(W)[:int(sizes[g])]
        e[:, g] = rng.choice(pool, (N, 16, W)); l[:, g, 1:] = rng.choice(pool, (N, 15, M))
    th[::2] = 4080; th[1::2] = 0
    return pack(X, e, l, z, th)
def setup_inputs_lull(rng):
    X = np.zeros((N, 8, 16, W), np.int64); e = np.zeros((N, 8, 16, W), np.int64); l = rng.integers(0, W, (N, 8, 16, M)); z = rng.integers(107, 149, (N, 8, 16, M))
    for g in range(8):
        o = rng.permutation(W); bar, grey = int(o[0]), int(o[1]); dl, dh, bl, bh = [o[2 + j::4] for j in range(4)]
        dark = np.concatenate([dl, dh]); bright = np.concatenate([bl, bh]); low = np.concatenate([dl, bl]); high = np.concatenate([dh, bh, o[:2]])
        x = X[:, g]; s = e[:, g]; m = l[:, g]; v = z[:, g]
        x[:, :, dark] = rng.integers(60, 101, (N, 16, len(dark))); x[:, :, bright] = rng.integers(155, 196, (N, 16, len(bright)))
        x[:, :, bar] = 255 * rng.integers(0, 2, (N, 16)); x[:, :, grey] = rng.integers(107, 149, (N, 16))
        s[:, :, low] = rng.choice(dark, (N, 16, len(low))); s[:, :, high] = rng.choice(bright, (N, 16, len(high)))
        s[:, 1, high] = rng.choice(bl, (N, len(high))); s[:, 2, high] = rng.choice(bh, (N, len(high)))
        np.put_along_axis(s, rng.integers(3, 15, (N, 1, W)), bar, 1)
        m[:, 0] = bar; m[:, 1] = np.stack([rng.permutation(low)[:M] for q in range(N)]); m[:, 2] = rng.choice(high[:-2], (N, M))
        m[:, 3:, 3::16] = grey; m[:, 4:, 11::16] = grey
        v[:, :, 3::16] = x[:, :, grey][:, :, None]; v[:, :, 11::16] = x[:, :, grey][:, :, None]
    th = np.zeros((N, 8), np.int64); th[::2] = rng.integers(1310, 1361, th[::2].shape); th[::2, rng.permutation(8)[:3]] = 4080
    return pack(X, e, l, z, th)
def check_inputs(d):
    bad = []
    for k, lo, hi in (("xt", 0, 255), ("ex", 0, W - 1), ("l0", 0, W - 1), ("z0", 0, 255), ("th", 0, 4080)):
        v = np.asarray(d[k]).astype(np.float64)
        if not (np.min(v) >= lo and np.max(v) <= hi): bad.append("range of " + k)
        elif not np.all(v == np.floor(v)): bad.append("whole numbers of " + k)
    return bad
def pick(w, ix):
    return np.take_along_axis(w, ix.reshape(8, 1, -1), 2).reshape((8, 16) + ix.shape[1:])
def at(l, k):
    return np.take_along_axis(l, k[:, None, :], 1)[:, 0]
def reference(xt, ex, l0, z0, th):
    X = xt.astype(np.float32).astype(np.int32).reshape(N, 8, 16, W); R = ex.astype(np.int64).reshape(N, 8, 16, W)
    L = l0.astype(np.int64).reshape(N, 8, 16, M); Z = z0.astype(np.float32).astype(np.int32).reshape(N, 8, 16, M); limit = th.astype(np.int64).reshape(N, 8, 1)
    count = [0] * N; kk = np.arange(16)[None, :, None]; gg = np.arange(8)[:, None] + np.zeros((8, M), np.int64); ii = np.arange(M)[None, :] + np.zeros((8, M), np.int64)
    for t in range(TV):
        for h in range(N):
            q = (h + S * t) % N; x = X[q]; l = L[h].copy(); z = Z[h].copy()
            d = np.add.reduce(np.abs(pick(x, l) - z[:, :, None, :]), axis=1).astype(np.int64)
            conf = np.any(pick(R[q], l) == l[:, None, :1, :], axis=1)
            key = np.where(conf, 2 ** 16 + kk, 16 * d + kk); key[:, 0] = 2 ** 20
            o = np.argsort(key, axis=1, kind="stable"); ra = o[:, 0]; rb = o[:, 1]
            la = at(l, ra); lb = at(l, rb); e = []
            Ea = pick(R[q], la); Eb = pick(R[q], lb)
            for E in (Ea, Eb):
                de = np.add.reduce(np.abs(pick(x, E) - z[:, :, None, :]), axis=1)
                e.append(at(E, np.argmin(de, axis=1)))
            far = 16 * d + 15 - kk; far[:, 0] = -1
            np.put_along_axis(far, ra[:, None, :], -1, 1); np.put_along_axis(far, rb[:, None, :], -1, 1)
            new = l.copy()
            for v in e:
                p = np.argmax(far, axis=1); np.put_along_axis(far, p[:, None, :], -1, 1); np.put_along_axis(new, p[:, None, :], v[:, None, :], 1)
            xa = pick(x, e[0]); xb = pick(x, e[1])
            acc = np.add.reduce(np.abs(xa - xb), axis=1) < limit[q] + (count[h] & 63)
            new[:, 1:] = np.where(acc[:, None, :], Eb[:, 1:], new[:, 1:])
            first = np.full((8, W), M); np.minimum.at(first, (gg[acc], la[acc]), ii[acc])
            win = acc & (first[gg, la] == ii)
            R[q][gg[win], (ii[win] + t) & 15, la[win]] = l[:, 0][win]
            L[h] = new; Z[h] = (xa + xb) >> 1; count[h] = int(np.count_nonzero(acc))
    home = [(q - S * (TV - 1)) % N for q in range(N)]
    return {"yl": L[home].reshape(N, 128, M).astype(np.float32), "yz": Z[home].reshape(N, 128, M).astype(np.float32).astype(BF),
            "yr": np.add.reduce(R.reshape(N, 128, B, W // B), axis=2).astype(np.float32)}

@@ -1,0 +1,601 @@
+from concourse.mybir import AluOpType, ActivationFunctionType
+
+A = AluOpType
+F = ActivationFunctionType
+N, W, M, TV = 4, 2048, 192, 6
+CW, NP = 96, 1536
+MW = 2 * CW + 6
+B20, B21, B22, B25, B26 = [float(2 ** k) for k in (20, 21, 22, 25, 26)]
+LV = ()
+SD_ = ()
+XV = ()
+BYS = (3, 4, 5, 8, 9, 10, 11)
+
+SCRATCH = {
+    "X": ("sbuf", [128, W], "bfloat16"), "Ri": ("sbuf", [128, W], "int32"), "R": ("sbuf", [128, W + M], "float32"), "RH": ("sbuf", [128, W], "float16"),
+    "l0i": ("sbuf", [128, M], "int32"), "thi": ("sbuf", [8, 1], "int32"), "thf": ("sbuf", [8, 1], "float32"), "G8": ("sbuf", [8, 128], "float32"),
+    "ylo": ("sbuf", [128, M], "float32"), "yro": ("sbuf", [128, 256], "float32"),
+}
+PLACE, DTY, END = {}, {}, {}
+
+
+def piece(buf, dtype, width, *names):
+    for name in names:
+        PLACE[name] = (buf, END.get(buf, 0))
+        DTY[name] = dtype
+        END[buf] = END.get(buf, 0) + (width + 15) // 16 * 16
+        SCRATCH[buf] = ("sbuf", [128, END[buf]], dtype)
+
+
+piece("AI", "int32", 2056, "IW")
+piece("AI", "int32", 208, "ICi", "I15i", "IGi")
+piece("AI", "int32", 24, "IPi", "ci", "ki", "BNi", "BEi", "BCi", "ni")
+piece("AI", "int32", 2 * M, "MN")
+piece("AH", "float16", M, "L0R0", "L0R1", "L0R2", "L0R3", "LH", "LR", "LK", "EAC")
+piece("AH", "float16", 2 * M, "PE2")
+piece("AH", "float16", NP, "SIH")
+piece("AH", "float16", 512, "PERM")
+piece("AH", "float16", 128, "IDH", "R0", "L0T0", "L0T1")
+piece("AF", "float32", NP, *["LX%d%d" % (k, c) for k in range(4) for c in range(2)])
+piece("AF", "float32", 208, "IC", "I15", "DM", "NM", "IG")
+piece("AF", "float32", M, "M2", "NCB", "DL", "SD", "tmp", "DZ", "NDZ", "MS", "LF", "DS", "NK", "FK", "KEEP", "EL", "IDF")
+piece("AF", "float32", 16 + M, "C1", "C2")
+piece("AF", "float32", 2 * M, "GM", "SE", "P12")
+piece("AF", "float32", CW, "CC")
+piece("AF", "float32", 32, "FH")
+piece("AF", "float32", 24, "LAM", "LMC", "ACA", "W2", "CI", "CJ", "cf", "nn", "ns", "TH", "THN")
+piece("AF", "float32", NP, "IXi")
+piece("AU", "uint16", 24, "BC", "BA", "BN", "BE", "LAMU", "WLU", "JL", "JP")
+piece("AU", "uint16", MW, *["LN%d%d" % (k, c) for k in range(TV) for c in range(2)])
+piece("AU", "uint16", MW, *["MG%d%d" % (k, c) for k in range(TV - 1) for c in range(2)])
+piece("AU", "uint16", M, "ZU")
+piece("AB", "bfloat16", 128, "IDB", "NIDB", "ID2", "BO", "LTR", "UTR", "ONE")
+piece("AB", "bfloat16", 2048, "SEL", "SELC")
+piece("AB", "bfloat16", NP, "SI")
+piece("AB", "bfloat16", M, "PDC", "PCC", "P2C", "Z", "zin", "yzo", "DA")
+piece("AB", "bfloat16", 2 * M, "dab")
+piece("AB", "bfloat16", 16, "B8", "AC2")
+piece("AB", "bfloat16", 1248, "EW")
+for c_ in "01":
+    piece("AF", "float32", M, "SG" + c_, "EDF" + c_)
+    piece("AH", "float16", M, "EA" + c_)
+    piece("AU", "uint16", 24, "KL" + c_)
+    piece("AU", "uint16", M, "EDU" + c_)
+    piece("AB", "bfloat16", 128, "ZT" + c_)
+    piece("AB", "bfloat16", NP, "XG" + c_, "AX" + c_, "EQ" + c_, "ZE" + c_)
+    piece("AB", "bfloat16", 2 * NP, "DAB" + c_, "AD" + c_)
+    SCRATCH["ET" + c_] = ("sbuf", [128, 6, 2, 16], "float16")
+    for n_ in ("XD", "PC", "PD"):
+        SCRATCH[n_ + c_] = ("psum", [128, 512], "float32")
+SCRATCH["ED"] = ("psum", [128, 16, 2, 16], "float32")
+SCRATCH["XD2"] = ("psum", [128, 512], "float32")
+LOADS = ["l0", "z0", "th", "ex0", "ex1", "xt"]
+SEMAPHORES = ["sV", "sS", "sP", "sG", "snt", "st"] + ["ld_" + k for k in LOADS] + ["ar%d%d" % (t, c) for t in range(1, TV) for c in range(2)] + ["al" + k for k in "123"]
+
+CYC, OVH, WAKE, NET = 0.00083 * 1.25, 0.03, 0.1, 3.5
+GATH, PEC = 1.55, 0.0005
+
+
+def is_psum(b):
+    return b in SCRATCH and SCRATCH[b][0] == "psum"
+
+
+def build(ops):
+    acc = {}
+    for i, o in enumerate(ops):
+        deps = set()
+        for wr, lst in ((0, o["r"]), (1, o["w"])):
+            for b, lo, hi in lst:
+                for (j, l2, h2, w2) in acc.get(b, ()):
+                    over = l2 < hi and lo < h2
+                    if (over and (wr or w2)) or (is_psum(b) and ops[j]["e"] != o["e"]):
+                        deps.add(j)
+        for wr, lst in ((0, o["r"]), (1, o["w"])):
+            for b, lo, hi in lst:
+                old = acc.setdefault(b, [])
+                if wr and not is_psum(b):
+                    old[:] = [x for x in old if not (lo <= x[1] and x[2] <= hi)]
+                old.append((i, lo, hi, wr))
+        if "after" in o:
+            deps.add(o["after"])
+        o["d"] = deps
+    return ops
+
+
+TICK, AMP, SEED = 0.1, 0.0, 1
+BON = [2.0, -5.0, -5.0, -5.0, -10.0, 0.0, 0.0, 0.0, -3.0, 10.0]
+
+
+def schedule(ops):
+    n = len(ops)
+    left = [len(o["d"]) for o in ops]
+    users = [[] for _ in ops]
+    for i, o in enumerate(ops):
+        for j in o["d"]:
+            users[j].append(i)
+    tail = [0.0] * n
+    for i in range(n - 1, -1, -1):
+        tail[i] = ops[i]["t"] + ops[i].get("lat", 0.0) + max([tail[j] + WAKE for j in users[i]] + [0.0])
+    x = SEED
+    for i in range(n):
+        x = (x * 1103515245 + 12345) % 2147483648
+        tail[i] += AMP * x / 2147483648.0 + BON[ops[i]["bi"]]
+    free, fin, order = {}, [0.0] * n, []
+    ready = [i for i in range(n) if left[i] == 0]
+    est = {i: 0.0 for i in ready}
+    while ready:
+        best = None
+        for i in ready:
+            e = ops[i]["e"]
+            s = max(est[i], free.get(e, 0.0)) if e != "net" else est[i]
+            key = (round(s / TICK), -tail[i], i)
+            if best is None or key < best[0]:
+                best = (key, i, s)
+        _, i, s = best
+        ready.remove(i)
+        e = ops[i]["e"]
+        fin[i] = s + ops[i]["t"] + ops[i].get("lat", 0.0)
+        ops[i]["s"] = s
+        free[e] = s + ops[i]["t"]
+        order.append(i)
+        for j in users[i]:
+            left[j] -= 1
+            est[j] = max(est.get(j, 0.0), fin[i] + (WAKE if ops[j]["e"] != e else 0.06))
+            if left[j] == 0:
+                ready.append(j)
+    order.sort(key=lambda i: (ops[i]["s"], i))
+    return order, max(fin)
+
+
+def program(g, core, T, topo):
+    ops = []
+    rank = T.rank_of(core)
+    bonus = [6]
+
+    def op(e, fns, r, w, t, **k):
+        o = {"e": e, "f": fns, "r": r, "w": w, "t": t, "bi": bonus[0]}
+        o.update(k)
+        ops.append(o)
+
+    def sl(x, p=128):
+        b, o = PLACE.get(x[0], (x[0], 0))
+        return T[b][0:p, o + x[1]:o + x[2]] if len(x) == 3 else T[b][0:p, o + x[1]:o + x[2]:x[3]]
+
+    def rg(x):
+        return (x[0], x[1], x[2])
+
+    def num(x):
+        return len(range(*x[1:]))
+
+    def two(x):
+        return (DTY[x[0]] if x[0] in DTY else SCRATCH[x[0]][2]) in ("bfloat16", "float16", "uint16")
+
+    def cyc(c):
+        return OVH + max(c, 64) * CYC
+
+    def copy(o, i, p=128):
+        op("V", [lambda: g.vector.tensor_copy(sl(o, p), sl(i, p))], [rg(i)], [rg(o)], cyc(num(o) * (0.5 if two(o) and two(i) else 1)))
+
+    def tt(o, a, b, f):
+        op("V", [lambda: g.vector.tensor_tensor(sl(o), sl(a), sl(b), f)], [rg(a), rg(b)], [rg(o)], cyc(num(o) * (1 if is_psum(a[0]) or is_psum(b[0]) else 2)))
+
+    def ts(o, a, s1, f1, s2=None, f2=None):
+        def run():
+            p, q = [sl(x) if isinstance(x, tuple) else x for x in (s1, s2)]
+            if f2 is None:
+                return g.vector.tensor_scalar(sl(o), sl(a), p, None, f1)
+            return g.vector.tensor_scalar(sl(o), sl(a), p, q, f1, f2)
+        op("V", [run], [rg(a)] + [rg(x) for x in (s1, s2) if isinstance(x, tuple)], [rg(o)], cyc(num(o) * (0.5 if two(o) and two(a) else 1)))
+
+    def scan(o, d0, d1, ini, f0, f1):
+        op("V", [lambda: g.vector.tensor_tensor_scan(sl(o), sl(d0), sl(d1), ini, f0, f1)], [rg(d0), rg(d1)], [rg(o)], cyc(num(o)))
+
+    def fill(o, v):
+        op("V", [lambda: g.vector.memset(sl(o), v)], [], [rg(o)], cyc(num(o) * (0.5 if two(o) else 1)))
+
+    def gath(o, w, off, other=None, f=None):
+        def run():
+            x = sl(w).indirect(sl(off))
+            return g.vector.tensor_copy(sl(o), x) if other is None else g.vector.tensor_tensor(sl(o), x, sl(other), f)
+        op("V", [run], [rg(w), rg(off)] + ([rg(other)] if other else []), [rg(o)], 0.05 + num(o) * GATH * CYC)
+
+    def act(o, i, f=F.Copy, scale=1.0, p=128, acc=None, bias=0.0):
+        def run():
+            if acc:
+                return g.scalar.activation(sl(o), sl(i), f, accum_out=sl(acc))
+            return g.scalar.activation(sl(o, p), sl(i, p), f, bias, scale)
+        op("S", [run], [rg(i)], [rg(o)] + ([rg(acc)] if acc else []), 0.1 + num(o) * CYC)
+
+    def sgath(o, w, off):
+        op("S", [lambda: g.scalar.activation(sl(o), sl(w).indirect(sl(off)), F.Copy)], [rg(w), rg(off)], [rg(o)], 0.07 + num(o) * GATH * CYC)
+
+    def mm(o, pairs, p=128, k96=()):
+        def mk(k, l, r):
+            q = 96 if k in k96 else 128
+            return lambda: g.tensor.matmul(sl(o, p), sl(l, q), sl(r, q), k == 0, k == len(pairs) - 1)
+        op("P", [mk(k, l, r) for k, (l, r) in enumerate(pairs)], [rg(x) for pr in pairs for x in pr], [rg(o)], 0.03 + len(pairs) * max(num(o), 64) * PEC)
+
+    def a2d(b0, et, nb):
+        b, o = PLACE["PERM"]
+
+        def one(v, y):
+            k = o + 128 * (2 * v + y)
+            return lambda: g.tensor.matmul(T.ED[:, b0:b0 + nb, v, :], T[b][:, k:k + 128], T[et][:, 0:nb, y, :], y == 0, y == 1)
+        op("P", [one(v, y) for v in range(2) for y in range(2)], [("PERM", 0, 512), (et, 0, 192)], [("ED", 32 * b0, 32 * (b0 + nb))], 0.03 + 4 * 96 * PEC)
+
+    def turn(et, x):
+        n = num(x) // 32
+        op("V", [lambda: g.vector.transpose(T[et][:, 0:n, :, :], sl(x))], [rg(x)], [(et, 0, 192)], cyc(16 * n))
+
+    def copy4(o, b0, b1):
+        op("V", [lambda: g.vector.tensor_copy(sl(o), T.ED[:, b0:b1, :, :])], [("ED", 32 * b0, 32 * b1)], [rg(o)], cyc(num(o)))
+
+    def act4(o, b0, b1, bias):
+        op("S", [lambda: g.scalar.activation(sl(o), T.ED[:, b0:b1, :, :], F.Copy, bias, 1.0)], [("ED", 32 * b0, 32 * b1)], [rg(o)], 0.1 + num(o) * CYC)
+
+    def load(out, i, sem, b, n, lo=0):
+        op("Y", [lambda: g.sync.dma_start(out, i)], [], [(b, lo, lo + n)], 0.1, lat=2.5, sem=("ld_" + sem, 16))
+
+    def store(out, x):
+        op("Y", [lambda: g.sync.dma_start(out[:], sl(x))], [rg(x)], [], 0.1, lat=2.0, sem=("st", 16))
+
+    def iota(x, pat, base, cm, fl=False):
+        op("G", [lambda: g.iota(sl(x), pat, base, cm, allow_small_or_imprecise_dtypes=True) if fl else g.iota(sl(x), pat, base, cm)], [], [rg(x)], 0.13 + num(x) * 2 * CYC)
+
+    def send(k, x, y, sem):
+        src, d = T.cores[(rank - k) % N], T.cores[(rank + k) % N]
+        rid, pid = topo.addr(d, core)
+        m = topo.mask(core, d)
+        op("G", [lambda: g.remote_dma(sl(y), sl(x), T.sem[sem], T.sem.snt, pid, rid, m)], [rg(x)], [], 0.6, send=len(topo.engines(core, d)))
+        op("net", [], [], [rg(y)], NET, sem=(sem, len(topo.engines(src, core))), after=len(ops) - 1)
+
+    load(T.l0i[:], T.l0[:], "l0", "l0i", M)
+    load(sl(("zin", 0, M)), T.z0[:], "z0", "zin", M)
+    load(T.X[:], T.xt[:], "xt", "X", W)
+    load(T.Ri[:, 0:1024], T.ex[:, 0:1024], "ex0", "Ri", 1024)
+    load(T.Ri[:, 1024:2048], T.ex[:, 1024:2048], "ex1", "Ri", 1024, 1024)
+    load(T.thi[:], T.th[:], "th", "thi", 1)
+    bonus[0] = 9
+    iota(("IPi", 0, 1), [[0, 1]], 0, 1)
+    iota(("ICi", 0, 208), [[1, 208]], 0, 0)
+    bonus[0] = 6
+    iota(("IXi", 0, NP), [[16, 6], [0, 16], [1, 16]], 0, 0, True)
+    iota(("BCi", 0, 12), [[16, 12]], 15, 0)
+    iota(("BNi", 0, 12), [[192, 2], [16, 6]], CW + 15, 0)
+    iota(("BEi", 0, 24), [[96, 2], [192, 2], [16, 6]], 15, 0)
+    iota(("IW", 0, 2056), [[1, 2056]], 0, 0)
+    bonus[0] = 9
+    PP, PU, PG, P0, P1, PZ, UM, UP, PX = [("cf", k, k + 1) for k in range(9)]
+    ts(("ci", 0, 1), ("IPi", 0, 1), 15, A.bitwise_and)
+    ts(("ci", 1, 2), ("IPi", 0, 1), 4, A.arith_shift_right)
+    ts(("ci", 2, 3), ("IPi", 0, 1), 4, A.arith_shift_right, 1, A.bitwise_and)
+    copy(PP, ("IPi", 0, 1))
+    copy(PU, ("ci", 0, 1))
+    copy(PG, ("ci", 1, 2))
+    copy(P1, ("ci", 2, 3))
+    copy(("IC", 0, 208), ("ICi", 0, 208))
+    ts(("IGi", 0, 128), ("ICi", 0, 128), 4, A.arith_shift_right)
+    copy(("IG", 0, 128), ("IGi", 0, 128))
+    ts(P0, P1, 0.0, A.is_equal)
+    ts(UM, PP, -16.0, A.add)
+    ts(UP, PP, 16.0, A.add)
+    IC1 = ("IC", 0, 128)
+    for v in range(2):
+        for y in range(2):
+            k = 128 * (2 * v + y)
+            ts(("PERM", k, k + 128), IC1, (UM, PP, UP)[y - v + 1], A.is_equal, P1 if v else P0, A.mult)
+    copy(("LH", 0, M), ("l0i", 0, M))
+    turn("ET0", ("LH", 0, M))
+    a2d(0, "ET0", 6)
+    copy4(("LN00", 0, CW), 0, 3)
+    copy4(("LN01", 0, CW), 3, 6)
+    ts(("B8", 0, 8), ("IC", 0, 8), PG, A.is_equal, 256.0, A.mult)
+    fill(("SEL", 0, 2048), 0.0)
+    ts(("BO", 0, 128), ("IG", 0, 128), PG, A.is_equal)
+    ts(PZ, PU, 0.0, A.is_equal)
+    ts(("R0", 0, 128), ("BO", 0, 128), PZ, A.mult)
+    ts(("IDH", 0, 128), IC1, PP, A.is_equal)
+    ts(("IDB", 0, 128), IC1, PP, A.is_equal)
+    ts(("IDF", 0, 128), IC1, PP, A.is_equal)
+    ts(("NIDB", 0, 128), IC1, PP, A.is_equal, -1.0, A.mult)
+    mm(("XD0", 0, M), [(("R0", 0, 128), ("LH", 0, M))])
+    copy(("L0R0", 0, M), ("XD0", 0, M))
+    for k in range(1, N):
+        send(k, ("L0R0", 0, M), ("L0R%d" % k, 0, M), "al%d" % k)
+    bonus[0] = 6
+    ts(("SI", 0, NP), ("IXi", 0, NP), PP, A.is_equal)
+    for u in range(16):
+        act(("SEL", 129 * u, 128 * u + 128, 16), ("B8", 0, 8))
+    act(("SELC", 0, 2048), ("SEL", 0, 2048), F.Copy, 4096.0)
+    copy(("SIH", 0, NP), ("SI", 0, NP))
+    ts(("I15i", 0, 208), ("ICi", 0, 208), 15, A.bitwise_and)
+    copy(("I15", 0, 208), ("I15i", 0, 208))
+    I15, tmp = ("I15", 0, M), ("tmp", 0, CW)
+    ts(("DZ", 0, M), I15, 0.0, A.is_equal, B22, A.mult)
+    ts(("NDZ", 0, M), ("DZ", 0, M), -1.0, A.mult)
+    ts(("MS", 0, M), I15, 0.0, A.is_gt)
+    ts(("DM", 0, 208), ("I15", 0, 208), PU, A.is_equal)
+    ts(("NM", 0, 208), ("I15", 0, 208), PU, A.not_equal)
+    ts(tmp, ("I15", 0, CW), -1.0, A.mult, 16.0, A.add)
+    ts(("CC", 0, CW), ("DZ", 0, CW), -16.0, A.mult)
+    tt(("PDC", 0, CW), tmp, ("CC", 0, CW), A.add)
+    tt(tmp, ("IC", 0, CW), ("I15", 0, CW), A.add)
+    ts(("CC", 0, CW), ("DZ", 0, CW), 16.5, A.mult, -16.0, A.add)
+    tt(("PCC", 0, CW), tmp, ("CC", 0, CW), A.add)
+    tt(tmp, ("IC", 0, CW), ("DZ", 0, CW), A.add)
+    ts(("CC", 0, CW), tmp, B20, A.add)
+    copy(("P2C", 0, M), ("IC", 0, M))
+    copy(("BC", 0, 12), ("BCi", 0, 12))
+    copy(("BN", 0, 12), ("BNi", 0, 12))
+    copy(("BE", 0, 24), ("BEi", 0, 24))
+    copy(("BA", 0, 24), ("ICi", 0, 24))
+    copy(("R", 0, 1024), ("Ri", 0, 1024))
+    copy(("R", 1024, 2048), ("Ri", 1024, 2048))
+    ts(("ID2", 0, 128), IC1, PP, A.is_equal, 2.0, A.mult)
+    ts(("tmp", 0, 128), IC1, PP, A.is_gt)
+    tt(("LTR", 0, 128), ("tmp", 0, 128), ("BO", 0, 128), A.mult)
+    tt(("UTR", 0, 128), ("BO", 0, 128), ("LTR", 0, 128), A.subtract)
+    fill(("ONE", 0, 128), 1.0)
+    ts(PX, PU, 2048.0, A.add)
+    ts(("CI", 0, 12), ("IC", 0, 12), 16.0, A.mult, PX, A.add)
+    ts(("CJ", 0, 12), ("CI", 0, 12), 1.0, A.add)
+    fill(("C1", 15, 16), B22)
+    fill(("C2", 15, 16), -B22)
+    op("V", [lambda: g.vector.tensor_copy(T.thf[:], T.thi[:])], [("thi", 0, 1)], [("thf", 0, 1)], cyc(1))
+    op("V", [lambda: g.vector.tensor_scalar(T.G8[:], sl(("IG", 0, 128), 8), sl(PP, 8), None, A.is_equal)], [("IG", 0, 128), PP], [("G8", 0, 128)], cyc(128))
+    op("P", [lambda: g.tensor.matmul(T.XD1[:, 0:1], T.G8[:], T.thf[:], True, True)], [("G8", 0, 128), ("thf", 0, 1)], [("XD1", 0, 1)], 0.1)
+    ts(("TH", 0, 1), ("XD1", 0, 1), 256.0, A.mult)
+    copy(("THN", 0, 1), ("TH", 0, 1))
+
+    SELS = [("SEL", 128 * u, 128 * u + 128) for u in range(16)]
+    SELK = [("SELC", 128 * u, 128 * u + 128) for u in range(16)]
+    IDB, NIDB, IDH = ("IDB", 0, 128), ("NIDB", 0, 128), ("IDH", 0, 128)
+    xd = [0]
+
+    def bank():
+        xd[0] = (xd[0] + 1) % 3
+        return "XD%d" % xd[0]
+
+    def l0x(t):
+        for c in range(2):
+            b = bank()
+            mm((b, 0, 128), [(("L0R%d" % t, CW * c, CW * c + CW), IDH)], p=96)
+            copy(("L0T%d" % c, 0, 128), (b, 0, 128), p=96)
+            for q in range(3):
+                b = bank()
+                mm((b, 0, 512), [(("L0T%d" % c, 0, 128), ("SIH", 512 * q, 512 * q + 512))], k96=(0,))
+                (copy if t and 3 * c + q in LV else act)(("LX%d%d" % (t, c), 512 * q, 512 * q + 512), (b, 0, 512))
+
+    def awayabs(out, raw, zt):
+        for q in range(3):
+            b = bank()
+            k = (512 * q, 512 * q + 512)
+            yield q
+            mm((b, 0, 512), [(NIDB, (raw[0], raw[1] + k[0], raw[1] + k[1])), ((zt, 0, 128), ("SI",) + k)], k96=(1,))
+            act((out[0], out[1] + k[0], out[1] + k[1]), (b, 0, 512), F.Abs)
+
+    def stage1(t, c):
+        s, LN = str(c), "LN%d%d" % (t, c)
+        j = (CW * c, CW * c + CW)
+        ZT, PC, PD = "ZT" + s, "PC" + s, "PD" + s
+        copy(("Z",) + j, (LN, CW, 2 * CW) if t else ("zin",) + j)
+        ts(("LF",) + j, (LN, 0, CW), 1.0, A.add)
+        mm((PD, 288, 416), [(("Z",) + j, IDB)], p=96)
+        act((ZT, 0, 128), (PD, 288, 416), p=96)
+        for q in awayabs(("AX" + s, 0), ("XG" + s, 0), ZT):
+            (gath if 3 * c + q in XV else sgath)(("XG" + s, 512 * q, 512 * q + 512), ("X", 0, W), (LN, 32 * q, 32 * q + 32))
+        gath(("EQ" + s, 0, NP), ("R", 0, W), (LN, 0, CW), ("LX%d%d" % (t % 4, c), 0, NP), A.is_equal)
+        mm((PD, 0, CW), [(SELS[u], ("AX" + s, u, NP, 16)) for u in range(16)] + [(IDB, ("PDC", 0, CW))])
+        act(("DS",) + j, (PD, 0, CW))
+        was = bonus[0]
+        bonus[0] = 8
+        mm((PC, 0, CW), [(SELK[u], ("EQ" + s, u, NP, 16)) for u in range(16)] + [(IDB, ("PCC", 0, CW))])
+        bonus[0] = was
+        NK, m0 = ("NK",) + j, 192 * c
+        tt((PC, 0, CW), (PC, 0, CW), ("DS",) + j, A.add)
+        tt(NK, (PC, 0, CW), ("CC", 0, CW), A.min)
+        scan(("MN", m0, m0 + CW), ("DZ", 0, CW), NK, B22, A.add, A.min)
+        tt(("C1", 16, 15 + CW), ("MN", m0, m0 + CW - 1), ("NK", j[0] + 1, j[1]), A.max)
+        scan(("MN", m0 + CW, m0 + M), ("DZ", 0, CW), ("C1", 15, 15 + CW), B22, A.add, A.min)
+        KL = "KL" + s
+        ki, GM = ("ki", 12 * c, 12 * c + 12), ("GM", m0, m0 + M)
+        ts(ki, ("MN", m0 + 15, m0 + M, 16), 255, A.bitwise_and)
+        copy((KL, 0, 12), ki)
+        gath(GM, ("LF",) + j, (KL, 0, 12), ("DM", 0, M), A.mult)
+        scan(("SG" + s, 0, M), ("MS", 0, M), GM, 0.0, A.mult, A.add)
+        ts((KL, 12, 24), ("SG" + s, 15, M, 16), -1.0, A.add)
+        gath(("EA" + s, 0, M), ("R", 0, W), (KL, 12, 24))
+        turn("ET" + s, ("EA" + s, 0, M))
+        a2d(6 * c, "ET" + s, 6)
+        copy4(("EDU" + s, 0, M), 6 * c, 6 * c + 6)
+        act4(("EDF" + s, 0, M), 6 * c, 6 * c + 6, 1.0)
+
+    def entries(t, c):
+        s = str(c)
+        for k in range(2):
+            for q in awayabs(("AD" + s, NP * k), ("DAB" + s, NP * k), "ZT" + s):
+                d = (NP * k + 512 * q, NP * k + 512 * q + 512)
+                (sgath if 6 * c + 3 * k + q in BYS else gath)(("DAB" + s,) + d, ("X", 0, W), ("EDU" + s, d[0] // 16, d[1] // 16))
+            o = CW + CW * k
+            mm(("PC" + s, o, o + CW), [(SELS[u], ("AD" + s, NP * k + u, NP * k + NP, 16)) for u in range(16)] + [(IDB, ("P2C", CW * k, CW * k + CW))])
+
+    def farthest(t, c):
+        j, w = (CW * c, CW * c + CW), (M * c, M * c + M)
+        PC, FK, FH = "PC%d" % c, ("FK",) + j, ("FH", 16 * c, 16 * c + 12)
+        BA, BB = ("BA", 0, 6), ("BA", 6, 12)
+        gath(("KEEP",) + j, ("MN", w[0] + CW, w[1]), ("BC", 0, 6), ("NK",) + j, A.is_lt)
+        tt(FK, ("PD%d" % c, 0, CW), ("KEEP",) + j, A.mult)
+        scan((PC, 288, 384), ("NDZ", 0, CW), FK, -B22, A.add, A.max)
+        tt(("C2", 16, 15 + CW), (PC, 288, 383), ("FK", j[0] + 1, j[1]), A.min)
+        scan((PC, 384, 480), ("NDZ", 0, CW), ("C2", 15, 15 + CW), -B22, A.add, A.max)
+        copy(FH, (PC, 303, 480, 16))
+        gath(("KEEP",) + j, FH, BB, FK, A.is_gt)
+        tt(("LK",) + j, ("KEEP",) + j, ("LF",) + j, A.mult)
+        gath(("P12", w[0], w[0] + CW), FH, BA, FK, A.is_equal)
+        gath(("P12", w[0] + CW, w[1]), FH, BB, FK, A.is_equal)
+
+    def tail(t, c):
+        s, j, w, k = str(c), (CW * c, CW * c + CW), (M * c, M * c + M), (12 * c, 12 * c + 12)
+        PD, PC = "PD" + s, "PC" + s
+        MG, nx = "MG%d%d" % (t, c), "LN%d%d" % (t + 1, c)
+        scan(("MN",) + w, ("DZ", 0, M), (PC, CW, 3 * CW), B22, A.add, A.min)
+        ts(("ki",) + k, ("MN", w[0] + 15, w[1], 16), 255, A.bitwise_and)
+        ts(("JP",) + k, ("ki",) + k, 16.0, A.mult, PU, A.add)
+        (sgath if c in SD_ else gath)(("dab",) + w, ("DAB" + s, 0, 2 * NP), ("JP",) + k)
+        copy(("JL",) + k, ("ki",) + k)
+        xa, xb = ("dab", w[0], w[0] + CW), ("dab", w[0] + CW, w[1])
+        mm((PC, 0, CW), [(IDB, xa), (NIDB, xb)])
+        mm((PD, CW, 2 * CW), [(IDB, xa), (IDB, xb)])
+        act(("DA",) + j, (PC, 0, CW), F.Abs)
+        mm((PC, 480, 486), [(SELS[u], ("DA", j[0] + u, j[1], 16)) for u in range(16)])
+        gath(("GM",) + w, ("EDF" + s, 0, M), ("JL",) + k, ("DM", 0, M), A.mult)
+        scan(("SE",) + w, ("MS", 0, M), ("GM",) + w, 0.0, A.mult, A.add)
+        gath(("PE2",) + w, ("SE",) + w, ("BC", 0, 12), ("P12",) + w, A.mult)
+        new = [(IDH, ("LK",) + j), (IDH, ("PE2", w[0], w[0] + CW)), (IDH, ("PE2", w[0] + CW, w[1]))]
+        mm((PD, 192, 288), new)
+        tt(("EL",) + j, ("EDF" + s, CW, M), (PD, 192, 288), A.subtract)
+        act(("EL", j[0], j[1], 16), ("EL", j[0], j[1], 16), F.Copy, 0.0)
+        AC, k = ("ACA", 8 * c, 8 * c + 6), (6 * c, 6 * c + 6)
+        ts(AC, (PC, 480, 486), ("THN", t, t + 1), A.is_lt)
+        gath(("EAC",) + j, AC, ("BA", 0, 6), ("EL",) + j, A.mult)
+        mm((PD, 192, 288), new + [(IDH, ("EAC",) + j)])
+        if t < TV - 1:
+            ts((MG, CW, 2 * CW), (PD, CW, 2 * CW), 0.5, A.mult, -0.25, A.add)
+            copy((MG, 2 * CW, MW), AC)
+            ts((MG, 0, CW), (PD, 192, 288), -1.0, A.add)
+            send(1, (MG, 0, MW), (nx, 0, MW), "ar%d%d" % (t + 1, c))
+        else:
+            ts(("ZU",) + j, (PD, CW, 2 * CW), 0.5, A.mult, -0.25, A.add)
+            copy(("yzo",) + j, ("ZU",) + j)
+            ts(("LK",) + j, (PD, 192, 288), -1.0, A.add)
+            turn("ET" + s, ("LK",) + j)
+            a2d(6 * c, "ET" + s, 3)
+            copy4(("ylo",) + j, 6 * c, 6 * c + 3)
+        e = ("SG" + s, 15, CW, 16)
+        tt(("LAM",) + k, e, AC, A.mult)
+        tt(("LMC",) + k, e, ("CJ",) + k, A.subtract)
+        tt(("LMC",) + k, ("LMC",) + k, AC, A.mult)
+        tt(("NCB",) + j, ("EA" + s, 0, CW), ("NM", j[0] + t, j[1] + t), A.mult)
+
+    def update(t):
+        copy(("LAMU", 0, 12), ("LAM", 0, 12))
+        gath(("LR", 0, M), ("IW", 0, 2056), ("LAMU", 0, 12))
+        at, pos = [], 0
+        for v in range(12):
+            n = M - 16 * v
+            ts(("EW", pos, pos + n), ("LR", 16 * v, M), ("LAM", v, v + 1), A.is_equal)
+            at.append(pos)
+            pos += n
+        fns, B = [], "PD1"
+
+        def one(l, lo, hi, p, st, sp):
+            return lambda: g.tensor.matmul(T[B][:, 288 + lo:288 + hi], sl((l, 0, 128)), sl(("EW", p, p + hi - lo)), st, sp)
+        fns.append(one("LTR", 0, M, 0, True, False))
+        fns.append(one("UTR", 16, M, 16, False, False))
+        for v in range(1, 12):
+            fns.append(one("LTR", 16 * v, 16 * v + 16, at[v], False, v == 11))
+            if v < 11:
+                fns.append(one("BO", 16 * v + 16, M, at[v] + 16, False, False))
+        op("P", fns, [("EW", 0, 1248), ("LTR", 0, 128), ("UTR", 0, 128), ("BO", 0, 128)], [(B, 288, 480)], 0.03 + 2200 * PEC)
+        tt(("DL", 0, M), (B, 288, 480), ("DM", 0, M), A.mult)
+        scan(("SD", 0, M), ("MS", 0, M), ("DL", 0, M), 0.0, A.mult, A.add)
+        W2 = ("W2", 0, 12)
+        ts(W2, ("SD", 15, M, 16), 0.5, A.is_lt)
+        tt(W2, W2, ("LMC", 0, 12), A.mult)
+        tt(W2, W2, ("CI", 0, 12), A.add)
+        copy(("WLU", 0, 12), W2)
+        op("V", [lambda: g.vector.tensor_tensor(T.R[:].indirect(sl(("WLU", 0, 12))), sl(("NCB", 0, M)), sl(("M2", 0, M)), A.add)],
+           [("WLU", 0, 12), ("NCB", 0, M), ("M2", 0, M)], [("R", 0, W + M)], 0.05 + M * 3.5 * CYC)
+
+    def count(t):
+        for c in range(2):
+            copy(("AC2", 6 * c, 6 * c + 6), ("LN%d%d" % (t, c), 2 * CW, MW))
+        mm(("PC0", 488, 500), [(("ONE", 0, 128), ("AC2", 0, 12))])
+        act(("nn", 0, 12), ("PC0", 488, 500), F.Copy, acc=("ns", 0, 1))
+        copy(("ni", 0, 1), ("ns", 0, 1))
+        ts(("ni", 0, 1), ("ni", 0, 1), 63, A.bitwise_and)
+        ts(("THN", t, t + 1), ("ni", 0, 1), 256.0, A.mult, ("TH", 0, 1), A.add)
+
+    l0x(0)
+    for t in range(TV):
+        bonus[0] = 0
+        stage1(t, 0)
+        bonus[0] = 1
+        tt(("M2", 0, M), ("DM", t, t + M), ("L0R%d" % (t % 4), 0, M), A.mult)
+        stage1(t, 1)
+        bonus[0] = 4
+        if t > 0:
+            count(t)
+        bonus[0] = 2
+        farthest(t, 0)
+        entries(t, 0)
+        bonus[0] = 3
+        farthest(t, 1)
+        entries(t, 1)
+        bonus[0] = 4
+        if t < 3:
+            l0x(t + 1)
+        bonus[0] = 7
+        tail(t, 0)
+        bonus[0] = 6
+        tail(t, 1)
+        bonus[0] = 5
+        update(t)
+        bonus[0] = 6
+    for h in range(3):
+        copy(("RH", 512 * h, 512 * h + 512), ("R", 512 * h, 512 * h + 512))
+    for h in range(4):
+        blocks = [("R", 1536, 1792), ("R", 1792, 2048)] if h == 0 else [("RH", 512 * h - 512, 512 * h - 256), ("RH", 512 * h - 256, 512 * h)]
+
+        def part(h, blocks):
+            return lambda k: g.tensor.matmul(T.XD0[:, 0:256], sl(("IDF" if h == 0 else "IDH", 0, 128)), sl(blocks[k]), h == 0 and k == 0, h == 3 and k == 1)
+
+        def call(f, k):
+            return lambda: f(k)
+        op("P", [call(part(h, blocks), k) for k in range(2)], [rg(b) for b in blocks] + [("IDF", 0, 128), IDH], [("XD0", 0, 256)], 2 * 256 * PEC * (4 if h == 0 else 1))
+    act(("yro", 0, 256), ("XD0", 0, 256))
+    store(T.yz, ("yzo", 0, M))
+    store(T.yl, ("ylo", 0, M))
+    store(T.yr, ("yro", 0, 256))
+    return build(ops)
+
+
+def rank_program(g, core, T, topo):
+    if T.rank_of(core) is None:
+        return
+    ops = program(g, core, T, topo)
+    order, _ = schedule(ops)
+    queue = {"V": g.vector, "S": g.scalar, "P": g.tensor, "G": g, "Y": g.sync}
+    own = {"V": "sV", "S": "sS", "P": "sP", "G": "sG"}
+    know = {k: {} for k in queue}
+    done, last = {}, {}
+    for i in order:
+        o = ops[i]
+        e = o["e"]
+        if e == "net":
+            s, v = o["sem"]
+            done[i], last[s] = (s, v, {s: v}), v
+            continue
+        kn = know[e]
+        for j in sorted(o["d"], key=lambda j: -ops[j]["s"]):
+            s, v, clk = done[j]
+            if kn.get(s, 0) < v:
+                queue[e].wait_ge(T.sem[s], v)
+            for a, b in clk.items():
+                if kn.get(a, 0) < b:
+                    kn[a] = b
+        if "send" in o:
+            for f in o["f"]:
+                f()
+            last["snt"] = last.get("snt", 0) + o["send"]
+            continue
+        s, k = o["sem"] if "sem" in o else (own[e], 1)
+        for f in o["f"]:
+            f().then_inc(T.sem[s], k)
+            last[s] = last.get(s, 0) + k
+        clk = dict(kn)
+        clk[s] = last[s]
+        done[i] = (s, last[s], clk)
+    for s, v in last.items():
+        if know["G"].get(s, 0) < v:
+            g.wait_ge(T.sem[s], v)

@@ -4,17 +4,26 @@ A = AluOpType
 F = ActivationFunctionType
 N, W, M, TV = 4, 2048, 192, 6
 CW, NP = 96, 1536
-MW = 2 * CW + 6
-B20, B21, B22, B25, B26 = [float(2 ** k) for k in (20, 21, 22, 25, 26)]
-LV = ()
-SD_ = ()
+MW = CW + 128
+RW = W + 2 * M
+K12, B25 = 4096.0, float(2 ** 25)
+XW, XN = 768, 2
+PU = "PT0"
 XV = ()
-BYS = (3, 4, 5, 8, 9, 10, 11)
+BYV = (0, 2, 4, 6)
+SD_ = (0, 1)
+SP_ = ()
+MX_ = (0,)
+LV0 = (3, 4, 5)
+BQ = 6
+CUT = 6
+TWICE = (1,)
+CF_ = (1,)
 
 SCRATCH = {
-    "X": ("sbuf", [128, W], "bfloat16"), "Ri": ("sbuf", [128, W], "int32"), "R": ("sbuf", [128, W + M], "float32"), "RH": ("sbuf", [128, W], "float16"),
+    "X": ("sbuf", [128, W], "bfloat16"), "Ri": ("sbuf", [128, W], "int32"), "R": ("sbuf", [128, RW], "float32"), "RH": ("sbuf", [128, W], "float16"),
     "l0i": ("sbuf", [128, M], "int32"), "thi": ("sbuf", [8, 1], "int32"), "thf": ("sbuf", [8, 1], "float32"), "G8": ("sbuf", [8, 128], "float32"),
-    "ylo": ("sbuf", [128, M], "float32"), "yro": ("sbuf", [128, 256], "float32"),
+    "ylo": ("sbuf", [128, M], "float32"), "yro": ("sbuf", [128, 256], "float32"), "DMB": ("sbuf", [128, 2 * NP], "bfloat16"),
 }
 PLACE, DTY, END = {}, {}, {}
 
@@ -27,52 +36,52 @@ def piece(buf, dtype, width, *names):
         SCRATCH[buf] = ("sbuf", [128, END[buf]], dtype)
 
 
-piece("AI", "int32", 2056, "IW")
-piece("AI", "int32", 208, "ICi", "I15i", "IGi")
-piece("AI", "int32", 24, "IPi", "ci", "ki", "BNi", "BEi", "BCi", "ni")
-piece("AI", "int32", 2 * M, "MN")
-piece("AH", "float16", M, "L0R0", "L0R1", "L0R2", "L0R3", "LH", "LR", "LK", "EAC")
-piece("AH", "float16", 2 * M, "PE2")
-piece("AH", "float16", NP, "SIH")
-piece("AH", "float16", 512, "PERM")
-piece("AH", "float16", 128, "IDH", "R0", "L0T0", "L0T1")
-piece("AF", "float32", NP, *["LX%d%d" % (k, c) for k in range(4) for c in range(2)])
+piece("AI", "int32", 24, "IPi", "ci", "BCi", "ni", "ki0", "ki1", "kj0", "kj1")
+piece("AI", "int32", 16, *["NS%d" % t for t in range(TV - 1)])
+piece("AI", "int32", 16, *["NL%d" % t for t in range(1, TV)])
+piece("AF", "float32", 2 * NP, "LX0", "LX1", "LX2", "LX3")
 piece("AF", "float32", 208, "IC", "I15", "DM", "NM", "IG")
-piece("AF", "float32", M, "M2", "NCB", "DL", "SD", "tmp", "DZ", "NDZ", "MS", "LF", "DS", "NK", "FK", "KEEP", "EL", "IDF")
-piece("AF", "float32", 16 + M, "C1", "C2")
-piece("AF", "float32", 2 * M, "GM", "SE", "P12")
+piece("AF", "float32", M, "L0R0", "L0R1", "L0R2", "L0R3", "M2", "NCB", "tmp", "DZ", "NDZ", "NK", "KEEP", "CIM", "DS", "IDF", "ONE")
+piece("AF", "float32", 16 + CW, "C1", "C2")
 piece("AF", "float32", CW, "CC")
-piece("AF", "float32", 32, "FH")
-piece("AF", "float32", 24, "LAM", "LMC", "ACA", "W2", "CI", "CJ", "cf", "nn", "ns", "TH", "THN")
-piece("AF", "float32", NP, "IXi")
-piece("AU", "uint16", 24, "BC", "BA", "BN", "BE", "LAMU", "WLU", "JL", "JP")
+piece("AF", "float32", 24, "cf", "DMR", "TH", "THN", "CNT")
+piece("AH", "float16", NP, "SIH")
+piece("AH", "float16", 144, "S1")
+piece("AH", "float16", 128, "IDH", "NIDH", "BOH", "R0", "HP", "HN", "L0T0", "L0T1")
+piece("AH", "float16", M, "LR", "WM")
+piece("AU", "uint16", 24, "BC", "WLU")
 piece("AU", "uint16", MW, *["LN%d%d" % (k, c) for k in range(TV) for c in range(2)])
 piece("AU", "uint16", MW, *["MG%d%d" % (k, c) for k in range(TV - 1) for c in range(2)])
 piece("AU", "uint16", M, "ZU")
-piece("AB", "bfloat16", 128, "IDB", "NIDB", "ID2", "BO", "LTR", "UTR", "ONE")
-piece("AB", "bfloat16", 2048, "SEL", "SELC")
-piece("AB", "bfloat16", NP, "SI")
-piece("AB", "bfloat16", M, "PDC", "PCC", "P2C", "Z", "zin", "yzo", "DA")
-piece("AB", "bfloat16", 2 * M, "dab")
-piece("AB", "bfloat16", 16, "B8", "AC2")
+piece("AB", "bfloat16", 128, "IDB", "NIDB", "HB", "N4K", "BO", "NBO", "BO4", "LTR", "UTR")
+piece("AB", "bfloat16", 144, "SK", "SC", "SH")
+piece("AB", "bfloat16", NP, "IX")
+piece("AB", "bfloat16", M, "PDC", "PCC", "PCD", "P2H", "P2L", "zin", "yzo", "DA", "SG", "C4K")
+piece("AB", "bfloat16", 16, "ACO")
 piece("AB", "bfloat16", 1248, "EW")
 for c_ in "01":
-    piece("AF", "float32", M, "SG" + c_, "EDF" + c_)
-    piece("AH", "float16", M, "EA" + c_)
-    piece("AU", "uint16", 24, "KL" + c_)
+    piece("AI", "int32", M, "MN" + c_)
+    piece("AI", "int32", 2 * M, "MT" + c_)
+    piece("AH", "float16", MW, "LV" + c_)
+    piece("AH", "float16", M, "ML" + c_, "EV" + c_, "ME" + c_, "Q" + c_, "EAC" + c_)
+    piece("AU", "uint16", 24, "KL" + c_, "JP" + c_)
     piece("AU", "uint16", M, "EDU" + c_)
-    piece("AB", "bfloat16", 128, "ZT" + c_)
-    piece("AB", "bfloat16", NP, "XG" + c_, "AX" + c_, "EQ" + c_, "ZE" + c_)
-    piece("AB", "bfloat16", 2 * NP, "DAB" + c_, "AD" + c_)
-    SCRATCH["ET" + c_] = ("sbuf", [128, 6, 2, 16], "float16")
-    for n_ in ("XD", "PC", "PD"):
-        SCRATCH[n_ + c_] = ("psum", [128, 512], "float32")
-SCRATCH["ED"] = ("psum", [128, 16, 2, 16], "float32")
-SCRATCH["XD2"] = ("psum", [128, 512], "float32")
-LOADS = ["l0", "z0", "th", "ex0", "ex1", "xt"]
-SEMAPHORES = ["sV", "sS", "sP", "sG", "snt", "st"] + ["ld_" + k for k in LOADS] + ["ar%d%d" % (t, c) for t in range(1, TV) for c in range(2)] + ["al" + k for k in "123"]
+    piece("AB", "bfloat16", MW, "dab" + c_)
+    piece("AB", "bfloat16", M, "P12" + c_)
+    piece("AB", "bfloat16", NP, "XG" + c_)
+    piece("AB", "bfloat16", 2 * NP, "DAB" + c_)
+    SCRATCH["AX" + c_] = ("sbuf", [128, 6, 256], "bfloat16")
+    SCRATCH["EQ" + c_] = ("sbuf", [128, 6, 256], "bfloat16")
+    SCRATCH["AD" + c_] = ("sbuf", [128, 12, 256], "bfloat16")
+for n_ in ("PK0", "PK1", "PT0", "PT1", PU):
+    SCRATCH[n_] = ("psum", [128, 512], "float32")
+for n_ in range(XN):
+    SCRATCH["XD%d" % n_] = ("psum", [128, (XW + 511) // 512 * 512], "float32")
+LOADS = ["l0", "z0", "th", "ex0", "ex1", "xt", "mb"]
+SEMAPHORES = (["sV", "sS", "sP", "sG", "snt", "st"] + ["ld_" + k for k in LOADS] + ["ar%d%d" % (t, c) for t in range(1, TV) for c in range(2)]
+              + ["al" + k for k in "123"] + ["an%d" % t for t in range(1, TV)])
 
-CYC, OVH, WAKE, NET = 0.00083 * 1.25, 0.03, 0.1, 3.5
+CYC, OVH, WAKE, SAME, NET = 0.00083 * 1.25, 0.03, 0.1, 0.06, 3.5
 GATH, PEC = 1.55, 0.0005
 
 
@@ -81,29 +90,65 @@ def is_psum(b):
 
 
 def build(ops):
-    acc = {}
+    acc, pe = {}, {}
     for i, o in enumerate(ops):
         deps = set()
         for wr, lst in ((0, o["r"]), (1, o["w"])):
             for b, lo, hi in lst:
                 for (j, l2, h2, w2) in acc.get(b, ()):
                     over = l2 < hi and lo < h2
+                    if o.get("apart") and ops[j].get("apart") == o["apart"]:
+                        continue
                     if (over and (wr or w2)) or (is_psum(b) and ops[j]["e"] != o["e"]):
                         deps.add(j)
         for wr, lst in ((0, o["r"]), (1, o["w"])):
             for b, lo, hi in lst:
                 old = acc.setdefault(b, [])
-                if wr and not is_psum(b):
+                if wr and not is_psum(b) and not o.get("apart"):
                     old[:] = [x for x in old if not (lo <= x[1] and x[2] <= hi)]
+                if is_psum(b) and o["e"] == "P":
+                    old[:] = []
                 old.append((i, lo, hi, wr))
         if "after" in o:
             deps.add(o["after"])
+        o["free"] = set()
+        if o["e"] == "P":
+            b = o["w"][0][0]
+            if b in pe and pe[b] not in deps:
+                o["free"].add(pe[b])
+                deps.add(pe[b])
+            if o.get("adds"):
+                o["free"] |= set(j for j in deps if ops[j]["e"] == "P")
+            pe[b] = i
         o["d"] = deps
     return ops
 
 
-TICK, AMP, SEED = 0.1, 0.0, 1
-BON = [2.0, -5.0, -5.0, -5.0, -10.0, 0.0, 0.0, 0.0, -3.0, 10.0]
+TICK, HOLD, LAM, ROUNDS = 0.05, 0.0, 2.0, 10
+BON = [0.0] * 9 + [-10.0, 0.0, 0.0]
+
+
+def lag(ops, j, i):
+    return WAKE if ops[j]["e"] != ops[i]["e"] else 0.0 if j in ops[i]["free"] or i in ops[j]["free"] else SAME
+
+
+def place(ops, order, before, back):
+    busy, start, fin = {}, {}, {}
+    for i in order:
+        o = ops[i]
+        lat = o.get("lat", 0.0)
+        s = max([fin[j] + lag(ops, j, i) for j in before[i]] + [0.0]) + (lat if back else 0.0)
+        if o["e"] != "net":
+            line = busy.setdefault(o["e"], [])
+            k = len(line)
+            while k and line[k - 1][1] > s:
+                k -= 1
+            while k < len(line) and line[k][0] < s + o["t"] - 1e-9:
+                s = max(s, line[k][1])
+                k += 1
+            line.insert(k, (s, s + o["t"]))
+        start[i], fin[i] = s, s + o["t"] + (0.0 if back else lat)
+    return start, fin
 
 
 def schedule(ops):
@@ -115,42 +160,40 @@ def schedule(ops):
             users[j].append(i)
     tail = [0.0] * n
     for i in range(n - 1, -1, -1):
-        tail[i] = ops[i]["t"] + ops[i].get("lat", 0.0) + max([tail[j] + WAKE for j in users[i]] + [0.0])
-    x = SEED
+        tail[i] = ops[i]["t"] + ops[i].get("lat", 0.0) + max([tail[j] + lag(ops, i, j) for j in users[i]] + [0.0])
     for i in range(n):
-        x = (x * 1103515245 + 12345) % 2147483648
-        tail[i] += AMP * x / 2147483648.0 + BON[ops[i]["bi"]]
-    free, fin, order = {}, [0.0] * n, []
+        tail[i] += BON[ops[i]["bi"]]
+    free, fin, at = {}, [0.0] * n, [0.0] * n
     ready = [i for i in range(n) if left[i] == 0]
     est = {i: 0.0 for i in ready}
     while ready:
-        best = None
-        for i in ready:
-            e = ops[i]["e"]
-            s = max(est[i], free.get(e, 0.0)) if e != "net" else est[i]
-            key = (round(s / TICK), -tail[i], i)
-            if best is None or key < best[0]:
-                best = (key, i, s)
-        _, i, s = best
+        start = {i: max(est[i], free.get(ops[i]["e"], 0.0)) if ops[i]["e"] != "net" else est[i] for i in ready}
+        f = min(ready, key=lambda i: (start[i] + HOLD * ops[i]["t"], i))
+        i = min([i for i in ready if ops[i]["e"] == ops[f]["e"] and start[i] <= start[f] + HOLD * ops[f]["t"] + TICK],
+                key=lambda i: (LAM * (start[i] - start[f]) - tail[i], i))
         ready.remove(i)
-        e = ops[i]["e"]
-        fin[i] = s + ops[i]["t"] + ops[i].get("lat", 0.0)
-        ops[i]["s"] = s
-        free[e] = s + ops[i]["t"]
-        order.append(i)
+        at[i], fin[i] = start[i], start[i] + ops[i]["t"] + ops[i].get("lat", 0.0)
+        free[ops[i]["e"]] = start[i] + ops[i]["t"]
         for j in users[i]:
             left[j] -= 1
-            est[j] = max(est.get(j, 0.0), fin[i] + (WAKE if ops[j]["e"] != e else 0.06))
+            est[j] = max(est.get(j, 0.0), fin[i] + lag(ops, i, j))
             if left[j] == 0:
                 ready.append(j)
-    order.sort(key=lambda i: (ops[i]["s"], i))
-    return order, max(fin)
+    best = (max(fin), at)
+    for _ in range(ROUNDS):
+        _, late = place(ops, sorted(range(n), key=lambda i: (-fin[i], -i)), users, True)
+        at, fin = place(ops, sorted(range(n), key=lambda i: (-late[i], i)), [o["d"] for o in ops], False)
+        if max(fin.values()) < best[0]:
+            best = (max(fin.values()), at)
+    for i in range(n):
+        ops[i]["s"] = best[1][i]
+    return sorted(range(n), key=lambda i: (ops[i]["s"], i)), best[0]
 
 
 def program(g, core, T, topo):
     ops = []
     rank = T.rank_of(core)
-    bonus = [6]
+    bonus = [0]
 
     def op(e, fns, r, w, t, **k):
         o = {"e": e, "f": fns, "r": r, "w": w, "t": t, "bi": bonus[0]}
@@ -158,6 +201,12 @@ def program(g, core, T, topo):
         ops.append(o)
 
     def sl(x, p=128):
+        if x[0] in SCRATCH and len(SCRATCH[x[0]][1]) == 3:
+            if len(x) == 3 and x[2] - x[1] == 256:
+                return T[x[0]][0:p, x[1] // 256, :]
+            if len(x) == 3:
+                return T[x[0]][0:p, x[1] // 256:x[2] // 256, :]
+            return T[x[0]][0:p, x[1] // 256:x[2] // 256, 16 * x[3]:16 * x[3] + 16]
         b, o = PLACE.get(x[0], (x[0], 0))
         return T[b][0:p, o + x[1]:o + x[2]] if len(x) == 3 else T[b][0:p, o + x[1]:o + x[2]:x[3]]
 
@@ -199,42 +248,25 @@ def program(g, core, T, topo):
             return g.vector.tensor_copy(sl(o), x) if other is None else g.vector.tensor_tensor(sl(o), x, sl(other), f)
         op("V", [run], [rg(w), rg(off)] + ([rg(other)] if other else []), [rg(o)], 0.05 + num(o) * GATH * CYC)
 
-    def act(o, i, f=F.Copy, scale=1.0, p=128, acc=None, bias=0.0):
-        def run():
-            if acc:
-                return g.scalar.activation(sl(o), sl(i), f, accum_out=sl(acc))
-            return g.scalar.activation(sl(o, p), sl(i, p), f, bias, scale)
-        op("S", [run], [rg(i)], [rg(o)] + ([rg(acc)] if acc else []), 0.1 + num(o) * CYC)
+    def act(o, i, f=F.Copy, scale=1.0, p=128, bias=0.0):
+        op("S", [lambda: g.scalar.activation(sl(o, p), sl(i, p), f, bias, scale)], [rg(i)], [rg(o)], 0.1 + num(o) * CYC)
 
     def sgath(o, w, off):
         op("S", [lambda: g.scalar.activation(sl(o), sl(w).indirect(sl(off)), F.Copy)], [rg(w), rg(off)], [rg(o)], 0.07 + num(o) * GATH * CYC)
 
-    def mm(o, pairs, p=128, k96=()):
-        def mk(k, l, r):
-            q = 96 if k in k96 else 128
-            return lambda: g.tensor.matmul(sl(o, p), sl(l, q), sl(r, q), k == 0, k == len(pairs) - 1)
-        op("P", [mk(k, l, r) for k, (l, r) in enumerate(pairs)], [rg(x) for pr in pairs for x in pr], [rg(o)], 0.03 + len(pairs) * max(num(o), 64) * PEC)
-
-    def a2d(b0, et, nb):
-        b, o = PLACE["PERM"]
-
-        def one(v, y):
-            k = o + 128 * (2 * v + y)
-            return lambda: g.tensor.matmul(T.ED[:, b0:b0 + nb, v, :], T[b][:, k:k + 128], T[et][:, 0:nb, y, :], y == 0, y == 1)
-        op("P", [one(v, y) for v in range(2) for y in range(2)], [("PERM", 0, 512), (et, 0, 192)], [("ED", 32 * b0, 32 * (b0 + nb))], 0.03 + 4 * 96 * PEC)
-
-    def turn(et, x):
-        n = num(x) // 32
-        op("V", [lambda: g.vector.transpose(T[et][:, 0:n, :, :], sl(x))], [rg(x)], [(et, 0, 192)], cyc(16 * n))
-
-    def copy4(o, b0, b1):
-        op("V", [lambda: g.vector.tensor_copy(sl(o), T.ED[:, b0:b1, :, :])], [("ED", 32 * b0, 32 * b1)], [rg(o)], cyc(num(o)))
-
-    def act4(o, b0, b1, bias):
-        op("S", [lambda: g.scalar.activation(sl(o), T.ED[:, b0:b1, :, :], F.Copy, bias, 1.0)], [("ED", 32 * b0, 32 * b1)], [rg(o)], 0.1 + num(o) * CYC)
+    def mm(o, terms, p=128, slow=1, first=True, last=True):
+        def mk(k, x):
+            q = x[2] if len(x) > 2 else 128
+            y = x[3] if len(x) > 3 else o
+            return lambda: g.tensor.matmul(sl(y, p), sl(x[0], q), sl(x[1], q), first and k == 0, last and k == len(terms) - 1)
+        step = 1 if num(o) > 256 else CUT
+        for k in range(0, len(terms), step):
+            part = terms[k:k + step]
+            op("P", [mk(k + n, x) for n, x in enumerate(part)], [rg(y) for x in part for y in x[:2]], [rg(o)],
+               slow * PEC * sum(max(num(x[3] if len(x) > 3 else o), 64) for x in part), adds=k > 0 or not first)
 
     def load(out, i, sem, b, n, lo=0):
-        op("Y", [lambda: g.sync.dma_start(out, i)], [], [(b, lo, lo + n)], 0.1, lat=2.5, sem=("ld_" + sem, 16))
+        op("Y", [lambda: g.sync.dma_start(out, i)], [], [(b, lo, lo + n)], 0.1, lat=2.5 + n / 1000.0, sem=("ld_" + sem, 16))
 
     def store(out, x):
         op("Y", [lambda: g.sync.dma_start(out[:], sl(x))], [rg(x)], [], 0.1, lat=2.0, sem=("st", 16))
@@ -249,310 +281,302 @@ def program(g, core, T, topo):
         op("G", [lambda: g.remote_dma(sl(y), sl(x), T.sem[sem], T.sem.snt, pid, rid, m)], [rg(x)], [], 0.6, send=len(topo.engines(core, d)))
         op("net", [], [], [rg(y)], NET, sem=(sem, len(topo.engines(src, core))), after=len(ops) - 1)
 
-    load(T.l0i[:], T.l0[:], "l0", "l0i", M)
-    load(sl(("zin", 0, M)), T.z0[:], "z0", "zin", M)
-    load(T.X[:], T.xt[:], "xt", "X", W)
-    load(T.Ri[:, 0:1024], T.ex[:, 0:1024], "ex0", "Ri", 1024)
-    load(T.Ri[:, 1024:2048], T.ex[:, 1024:2048], "ex1", "Ri", 1024, 1024)
-    load(T.thi[:], T.th[:], "th", "thi", 1)
-    bonus[0] = 9
-    iota(("IPi", 0, 1), [[0, 1]], 0, 1)
-    iota(("ICi", 0, 208), [[1, 208]], 0, 0)
-    bonus[0] = 6
-    iota(("IXi", 0, NP), [[16, 6], [0, 16], [1, 16]], 0, 0, True)
-    iota(("BCi", 0, 12), [[16, 12]], 15, 0)
-    iota(("BNi", 0, 12), [[192, 2], [16, 6]], CW + 15, 0)
-    iota(("BEi", 0, 24), [[96, 2], [192, 2], [16, 6]], 15, 0)
-    iota(("IW", 0, 2056), [[1, 2056]], 0, 0)
-    bonus[0] = 9
-    PP, PU, PG, P0, P1, PZ, UM, UP, PX = [("cf", k, k + 1) for k in range(9)]
-    ts(("ci", 0, 1), ("IPi", 0, 1), 15, A.bitwise_and)
-    ts(("ci", 1, 2), ("IPi", 0, 1), 4, A.arith_shift_right)
-    ts(("ci", 2, 3), ("IPi", 0, 1), 4, A.arith_shift_right, 1, A.bitwise_and)
-    copy(PP, ("IPi", 0, 1))
-    copy(PU, ("ci", 0, 1))
-    copy(PG, ("ci", 1, 2))
-    copy(P1, ("ci", 2, 3))
-    copy(("IC", 0, 208), ("ICi", 0, 208))
-    ts(("IGi", 0, 128), ("ICi", 0, 128), 4, A.arith_shift_right)
-    copy(("IG", 0, 128), ("IGi", 0, 128))
-    ts(P0, P1, 0.0, A.is_equal)
-    ts(UM, PP, -16.0, A.add)
-    ts(UP, PP, 16.0, A.add)
-    IC1 = ("IC", 0, 128)
-    for v in range(2):
-        for y in range(2):
-            k = 128 * (2 * v + y)
-            ts(("PERM", k, k + 128), IC1, (UM, PP, UP)[y - v + 1], A.is_equal, P1 if v else P0, A.mult)
-    copy(("LH", 0, M), ("l0i", 0, M))
-    turn("ET0", ("LH", 0, M))
-    a2d(0, "ET0", 6)
-    copy4(("LN00", 0, CW), 0, 3)
-    copy4(("LN01", 0, CW), 3, 6)
-    ts(("B8", 0, 8), ("IC", 0, 8), PG, A.is_equal, 256.0, A.mult)
-    fill(("SEL", 0, 2048), 0.0)
-    ts(("BO", 0, 128), ("IG", 0, 128), PG, A.is_equal)
-    ts(PZ, PU, 0.0, A.is_equal)
-    ts(("R0", 0, 128), ("BO", 0, 128), PZ, A.mult)
-    ts(("IDH", 0, 128), IC1, PP, A.is_equal)
-    ts(("IDB", 0, 128), IC1, PP, A.is_equal)
-    ts(("IDF", 0, 128), IC1, PP, A.is_equal)
-    ts(("NIDB", 0, 128), IC1, PP, A.is_equal, -1.0, A.mult)
-    mm(("XD0", 0, M), [(("R0", 0, 128), ("LH", 0, M))])
-    copy(("L0R0", 0, M), ("XD0", 0, M))
-    for k in range(1, N):
-        send(k, ("L0R0", 0, M), ("L0R%d" % k, 0, M), "al%d" % k)
-    bonus[0] = 6
-    ts(("SI", 0, NP), ("IXi", 0, NP), PP, A.is_equal)
-    for u in range(16):
-        act(("SEL", 129 * u, 128 * u + 128, 16), ("B8", 0, 8))
-    act(("SELC", 0, 2048), ("SEL", 0, 2048), F.Copy, 4096.0)
-    copy(("SIH", 0, NP), ("SI", 0, NP))
-    ts(("I15i", 0, 208), ("ICi", 0, 208), 15, A.bitwise_and)
-    copy(("I15", 0, 208), ("I15i", 0, 208))
-    I15, tmp = ("I15", 0, M), ("tmp", 0, CW)
-    ts(("DZ", 0, M), I15, 0.0, A.is_equal, B22, A.mult)
-    ts(("NDZ", 0, M), ("DZ", 0, M), -1.0, A.mult)
-    ts(("MS", 0, M), I15, 0.0, A.is_gt)
-    ts(("DM", 0, 208), ("I15", 0, 208), PU, A.is_equal)
-    ts(("NM", 0, 208), ("I15", 0, 208), PU, A.not_equal)
-    ts(tmp, ("I15", 0, CW), -1.0, A.mult, 16.0, A.add)
-    ts(("CC", 0, CW), ("DZ", 0, CW), -16.0, A.mult)
-    tt(("PDC", 0, CW), tmp, ("CC", 0, CW), A.add)
-    tt(tmp, ("IC", 0, CW), ("I15", 0, CW), A.add)
-    ts(("CC", 0, CW), ("DZ", 0, CW), 16.5, A.mult, -16.0, A.add)
-    tt(("PCC", 0, CW), tmp, ("CC", 0, CW), A.add)
-    tt(tmp, ("IC", 0, CW), ("DZ", 0, CW), A.add)
-    ts(("CC", 0, CW), tmp, B20, A.add)
-    copy(("P2C", 0, M), ("IC", 0, M))
-    copy(("BC", 0, 12), ("BCi", 0, 12))
-    copy(("BN", 0, 12), ("BNi", 0, 12))
-    copy(("BE", 0, 24), ("BEi", 0, 24))
-    copy(("BA", 0, 24), ("ICi", 0, 24))
-    copy(("R", 0, 1024), ("Ri", 0, 1024))
-    copy(("R", 1024, 2048), ("Ri", 1024, 2048))
-    ts(("ID2", 0, 128), IC1, PP, A.is_equal, 2.0, A.mult)
-    ts(("tmp", 0, 128), IC1, PP, A.is_gt)
-    tt(("LTR", 0, 128), ("tmp", 0, 128), ("BO", 0, 128), A.mult)
-    tt(("UTR", 0, 128), ("BO", 0, 128), ("LTR", 0, 128), A.subtract)
-    fill(("ONE", 0, 128), 1.0)
-    ts(PX, PU, 2048.0, A.add)
-    ts(("CI", 0, 12), ("IC", 0, 12), 16.0, A.mult, PX, A.add)
-    ts(("CJ", 0, 12), ("CI", 0, 12), 1.0, A.add)
-    fill(("C1", 15, 16), B22)
-    fill(("C2", 15, 16), -B22)
-    op("V", [lambda: g.vector.tensor_copy(T.thf[:], T.thi[:])], [("thi", 0, 1)], [("thf", 0, 1)], cyc(1))
-    op("V", [lambda: g.vector.tensor_scalar(T.G8[:], sl(("IG", 0, 128), 8), sl(PP, 8), None, A.is_equal)], [("IG", 0, 128), PP], [("G8", 0, 128)], cyc(128))
-    op("P", [lambda: g.tensor.matmul(T.XD1[:, 0:1], T.G8[:], T.thf[:], True, True)], [("G8", 0, 128), ("thf", 0, 1)], [("XD1", 0, 1)], 0.1)
-    ts(("TH", 0, 1), ("XD1", 0, 1), 256.0, A.mult)
-    copy(("THN", 0, 1), ("TH", 0, 1))
+    def sel(name, u):
+        return (name, 15 - u, 143 - u)
 
-    SELS = [("SEL", 128 * u, 128 * u + 128) for u in range(16)]
-    SELK = [("SELC", 128 * u, 128 * u + 128) for u in range(16)]
-    IDB, NIDB, IDH = ("IDB", 0, 128), ("NIDB", 0, 128), ("IDH", 0, 128)
     xd = [0]
 
     def bank():
-        xd[0] = (xd[0] + 1) % 3
+        xd[0] = (xd[0] + 1) % XN
         return "XD%d" % xd[0]
 
-    def l0x(t):
-        for c in range(2):
-            b = bank()
-            mm((b, 0, 128), [(("L0R%d" % t, CW * c, CW * c + CW), IDH)], p=96)
-            copy(("L0T%d" % c, 0, 128), (b, 0, 128), p=96)
-            for q in range(3):
-                b = bank()
-                mm((b, 0, 512), [(("L0T%d" % c, 0, 128), ("SIH", 512 * q, 512 * q + 512))], k96=(0,))
-                (copy if t and 3 * c + q in LV else act)(("LX%d%d" % (t, c), 512 * q, 512 * q + 512), (b, 0, 512))
-
-    def awayabs(out, raw, zt):
+    load(T.l0i[:], T.l0[:], "l0", "l0i", M)
+    load(T.X[:], T.xt[:], "xt", "X", W)
+    load(sl(("zin", 0, M)), T.z0[:], "z0", "zin", M)
+    load(T.Ri[:, 0:1024], T.ex[:, 0:1024], "ex0", "Ri", 1024)
+    load(T.Ri[:, 1024:2048], T.ex[:, 1024:2048], "ex1", "Ri", 1024, 1024)
+    load(T.thi[:], T.th[:], "th", "thi", 1)
+    iota(("IPi", 0, 1), [[0, 1]], 0, 1)
+    iota(("IC", 0, 144), [[1, 144]], 0, 0, True)
+    iota(("IG", 0, M), [[1, 12], [0, 16]], 0, 0, True)
+    for q in range(3):
+        iota(("IX", 512 * q, 512 * q + 512), [[1, 32], [0, 16]], 32 * q, 0, True)
+    iota(("I15", 0, 208), [[0, 13], [1, 16]], 0, 0, True)
+    iota(("BCi", 0, 6), [[16, 6]], 15, 0)
+    iota(("CIM", 0, M), [[2, M]], W, 0, True)
+    PP, PG0, PG, PZ, NZ, PE, PR, P16 = [("cf", k, k + 1) for k in range(8)]
+    ts(("ci", 0, 1), ("IPi", 0, 1), 15, A.bitwise_and)
+    ts(("ci", 1, 2), ("IPi", 0, 1), 4, A.arith_shift_right)
+    copy(PP, ("IPi", 0, 1))
+    copy(("cf", 1, 3), ("ci", 0, 2))
+    IC1, I15, tmp = ("IC", 0, 128), ("I15", 0, M), ("tmp", 0, CW)
+    IDB, NIDB, IDH, NIDH, HB, BO, BOH, R0, HP, HN = [(k, 0, 128) for k in ("IDB", "NIDB", "IDH", "NIDH", "HB", "BO", "BOH", "R0", "HP", "HN")]
+    ts(PZ, PG0, 0.0, A.is_equal)
+    ts(NZ, PG0, 0.0, A.is_gt)
+    ts(PE, PG, 16.0, A.mult, 15.0, A.add)
+    ts(PR, PG0, -1.0, A.mult, 16.0, A.add)
+    ts(P16, PG0, 16.0, A.mult)
+    ts(IDB, IC1, PP, A.is_equal)
+    act(NIDB, IDB, F.Copy, -1.0)
+    act(HB, IDB, F.Copy, 0.5)
+    act(("N4K", 0, 128), IDB, F.Copy, -K12)
+    act(("IDF", 0, 128), IDB)
+    copy(IDH, IDB)
+    ts(NIDH, IDB, -1.0, A.mult)
+    ts(HP, IDB, NZ, A.mult)
+    ts(HN, HP, -1.0, A.mult)
+    ts(BO, ("IG", 0, 128), PG, A.is_equal)
+    copy(BOH, BO)
+    ts(R0, BO, PZ, A.mult)
+    act(("BO4", 0, 128), BO, F.Copy, K12)
+    act(("NBO", 0, 128), BO, F.Copy, -1.0)
+    ts(("UTR", 0, 128), IC1, PP, A.is_gt)
+    tt(("LTR", 0, 128), ("UTR", 0, 128), ("BO4", 0, 128), A.mult)
+    for q in range(3):
+        ts(("SIH", 512 * q, 512 * q + 512), ("IX", 512 * q, 512 * q + 512), PP, A.is_equal)
+    ts(("SK", 0, 144), ("IC", 0, 144), PE, A.is_equal, K12, A.mult)
+    act(("SC", 0, 144), ("SK", 0, 144), F.Copy, K12)
+    act(("SH", 0, 144), ("SK", 0, 144), F.Copy, 1.0 / (16 * K12))
+    ts(("S1", 0, 144), ("SK", 0, 144), 1.0 / K12, A.mult)
+    ts(("DZ", 0, M), I15, 0.0, A.is_equal, B25, A.mult)
+    act(("NDZ", 0, CW), ("DZ", 0, CW), F.Copy, -1.0)
+    ts(("DM", 0, 208), ("I15", 0, 208), PG0, A.is_equal)
+    act(("NM", 0, 208), ("DM", 0, 208), F.Copy, -1.0, bias=1.0)
+    ts(("DMR", 0, 16), ("IC", 0, 16), PR, A.is_equal)
+    act(("DMB", 0, M), ("DM", 0, M))
+    op("Y", [(lambda k: lambda: g.sync.dma_start(T.DMB[:, M * k:M * k + M], T.DMB[:, 0:M]))(k) for k in range(1, 16)], [("DMB", 0, M)], [("DMB", M, 2 * NP)],
+       1.5, lat=3.0, sem=("ld_mb", 16))
+    act(tmp, ("I15", 0, CW), F.Copy, -1.0, bias=16.0)
+    tt(("PDC", 0, CW), tmp, ("NDZ", 0, CW), A.add)
+    if TWICE:
+        tt(("PCC", 0, CW), ("I15", 0, CW), ("DZ", 0, CW), A.add)
+    if len(TWICE) < 2:
+        act(("CC", 0, CW), ("DZ", 0, CW), F.Copy, 2.0, bias=-16.0)
+        act(tmp, ("I15", 0, CW), F.Copy, 2.0)
+        tt(("PCD", 0, CW), tmp, ("CC", 0, CW), A.add)
+    act(tmp, ("DZ", 0, CW), F.Copy, K12 / B25, bias=4081 * K12)
+    tt(("CC", 0, CW), tmp, ("I15", 0, CW), A.add)
+    act(("P2H", 0, M), ("IG", 0, M), F.Copy, 256.0)
+    ts(("P2L", 0, CW), ("I15", 0, CW), P16, A.add)
+    copy(("BC", 0, 6), ("BCi", 0, 6))
+    tt(("CIM", 0, M), ("CIM", 0, M), ("DM", 0, M), A.mult)
+    fill(("C4K", 0, M), K12)
+    fill(("ONE", 0, 128), 1.0)
+    fill(("C1", 15, 16), B25)
+    fill(("C2", 15, 16), -B25)
+    for c in "01":
+        fill(("dab" + c, M, MW), 0.0)
+    op("V", [lambda: g.vector.tensor_copy(T.thf[:], T.thi[:])], [("thi", 0, 1)], [("thf", 0, 1)], cyc(1))
+    op("V", [lambda: g.vector.tensor_scalar(T.G8[:], sl(("IG", 0, 128), 8), sl(PP, 8), None, A.is_equal)], [("IG", 0, 128), PP], [("G8", 0, 128)], cyc(128))
+    op("P", [lambda: g.tensor.matmul(T.PK1[:, 504:505], T.G8[:], T.thf[:], True, True)], [("G8", 0, 128), ("thf", 0, 1)], [("PK1", 504, 505)], 0.1)
+    copy(("TH", 0, 1), ("PK1", 504, 505))
+    bonus[0] = 11
+    for c in range(2):
+        j, LV, L0T = (CW * c, CW * c + CW), "LV%d" % c, ("L0T%d" % c, 0, 128)
+        copy(("LN0%d" % c, 0, CW), ("l0i",) + j)
+        copy((LV, 0, CW), ("l0i",) + j)
+        mm(("PT%d" % c, 0, 128), [(("zin",) + j, IDB)], p=96)
+        copy((LV, CW, MW), ("PT%d" % c, 0, 128), p=96)
+        mm(("PT%d" % c, 128, 256), [((LV, 0, CW), R0)], p=96)
+        copy(L0T, ("PT%d" % c, 128, 256), p=96)
         for q in range(3):
+            b = ("PK%d" % c, "PT%d" % c)[q % 2]
+            mm((b, 0, 512), [(L0T, ("SIH", 512 * q, 512 * q + 512), 96)])
+            (copy if 3 * c + q in LV0 else act)(("LX0", NP * c + 512 * q, NP * c + 512 * q + 512), (b, 0, 512))
+
+    def spread(k):
+        def one(r):
+            return lambda: g.affine_select(sl(("LX%d" % k, r, 2 * NP, 16)), sl(("L0R%d" % k, 0, M)), [[0, M]], A.is_ge, 0.0, 0, 0)
+        for r in range(16):
+            op("G", [one(r)], [("L0R%d" % k, 0, M)], [("LX%d" % k, 0, 2 * NP)], 0.17 + 2 * M * CYC, apart="LX%d" % k)
+
+    def awayabs(out, raw, lv, o):
+        for q in range(NP // XW):
             b = bank()
-            k = (512 * q, 512 * q + 512)
+            k = XW * q
             yield q
-            mm((b, 0, 512), [(NIDB, (raw[0], raw[1] + k[0], raw[1] + k[1])), ((zt, 0, 128), ("SI",) + k)], k96=(1,))
-            act((out[0], out[1] + k[0], out[1] + k[1]), (b, 0, 512), F.Abs)
+            for lo in range(0, XW, 512):
+                hi = min(XW, lo + 512)
+                mm((b, lo, hi), [((lv, CW, MW), ("SIH", k + lo, k + hi), 96), (NIDB, (raw, o + k + lo, o + k + hi))])
+            act((out, o + k, o + k + XW), (b, 0, XW), F.Abs)
 
     def stage1(t, c):
         s, LN = str(c), "LN%d%d" % (t, c)
         j = (CW * c, CW * c + CW)
-        ZT, PC, PD = "ZT" + s, "PC" + s, "PD" + s
-        copy(("Z",) + j, (LN, CW, 2 * CW) if t else ("zin",) + j)
-        ts(("LF",) + j, (LN, 0, CW), 1.0, A.add)
-        mm((PD, 288, 416), [(("Z",) + j, IDB)], p=96)
-        act((ZT, 0, 128), (PD, 288, 416), p=96)
-        for q in awayabs(("AX" + s, 0), ("XG" + s, 0), ZT):
-            (gath if 3 * c + q in XV else sgath)(("XG" + s, 512 * q, 512 * q + 512), ("X", 0, W), (LN, 32 * q, 32 * q + 32))
-        gath(("EQ" + s, 0, NP), ("R", 0, W), (LN, 0, CW), ("LX%d%d" % (t % 4, c), 0, NP), A.is_equal)
-        mm((PD, 0, CW), [(SELS[u], ("AX" + s, u, NP, 16)) for u in range(16)] + [(IDB, ("PDC", 0, CW))])
-        act(("DS",) + j, (PD, 0, CW))
-        was = bonus[0]
-        bonus[0] = 8
-        mm((PC, 0, CW), [(SELK[u], ("EQ" + s, u, NP, 16)) for u in range(16)] + [(IDB, ("PCC", 0, CW))])
-        bonus[0] = was
-        NK, m0 = ("NK",) + j, 192 * c
-        tt((PC, 0, CW), (PC, 0, CW), ("DS",) + j, A.add)
-        tt(NK, (PC, 0, CW), ("CC", 0, CW), A.min)
-        scan(("MN", m0, m0 + CW), ("DZ", 0, CW), NK, B22, A.add, A.min)
-        tt(("C1", 16, 15 + CW), ("MN", m0, m0 + CW - 1), ("NK", j[0] + 1, j[1]), A.max)
-        scan(("MN", m0 + CW, m0 + M), ("DZ", 0, CW), ("C1", 15, 15 + CW), B22, A.add, A.min)
-        KL = "KL" + s
-        ki, GM = ("ki", 12 * c, 12 * c + 12), ("GM", m0, m0 + M)
-        ts(ki, ("MN", m0 + 15, m0 + M, 16), 255, A.bitwise_and)
-        copy((KL, 0, 12), ki)
-        gath(GM, ("LF",) + j, (KL, 0, 12), ("DM", 0, M), A.mult)
-        scan(("SG" + s, 0, M), ("MS", 0, M), GM, 0.0, A.mult, A.add)
-        ts((KL, 12, 24), ("SG" + s, 15, M, 16), -1.0, A.add)
-        gath(("EA" + s, 0, M), ("R", 0, W), (KL, 12, 24))
-        turn("ET" + s, ("EA" + s, 0, M))
-        a2d(6 * c, "ET" + s, 6)
-        copy4(("EDU" + s, 0, M), 6 * c, 6 * c + 6)
-        act4(("EDF" + s, 0, M), 6 * c, 6 * c + 6, 1.0)
+        PK, LV, MN, KL, ML, RT = "PK" + s, "LV" + s, "MN" + s, "KL" + s, "ML" + s, ("R" if t else "Ri", 0, W)
+        if t:
+            copy((LV, 0, MW), (LN, 0, MW))
+        for q in awayabs("AX" + s, "XG" + s, LV, 0):
+            (gath if NP // XW * c + q in XV else sgath)(("XG" + s, XW * q, XW * q + XW), ("X", 0, W), (LN, XW * q // 16, XW * (q + 1) // 16))
+        for q in range(BQ):
+            k = (NP * q // BQ, NP * (q + 1) // BQ)
+            gath(("EQ" + s,) + k, RT, (LN, k[0] // 16, k[1] // 16), ("LX%d" % (t % 4), NP * c + k[0], NP * c + k[1]), A.is_equal)
+        dist = [(sel("SK", u), ("AX" + s, 0, NP, u)) for u in range(16)]
+        conf = [(sel("SC", u), ("EQ" + s, 0, NP, u)) for u in range(16)]
+        PD, PC, NK = (PK, 0, CW), (PK, CW, M), ("NK",) + j
+        if c in TWICE and c in CF_:
+            mm(PC, [(IDB, ("PCC", 0, CW))] + conf + dist)
+            mm(PD, [(IDB, ("PDC", 0, CW))] + dist)
+        elif c in TWICE:
+            mm(PD, [(IDB, ("PDC", 0, CW))] + dist)
+            mm(PC, [(IDB, ("PCC", 0, CW))] + dist + conf)
+        else:
+            mm(PD, [(IDB, ("PDC", 0, CW))] + dist)
+            act(("DS",) + j, PD)
+            mm(PC, [(IDB, ("PCD", 0, CW))] + conf)
+            tt(PC, PC, ("DS",) + j, A.add)
+        tt(NK, PC, ("CC", 0, CW), A.min)
+        scan((MN, 0, CW), ("DZ", 0, CW), NK, B25, A.add, A.min)
+        tt(("C1", 16, 15 + CW), (MN, 0, CW - 1), ("NK", j[0] + 1, j[1]), A.max)
+        scan((MN, CW, M), ("DZ", 0, CW), ("C1", 15, 15 + CW), B25, A.add, A.min)
+        ts(("ki" + s, 0, 12), (MN, 15, M, 16), 4095, A.bitwise_and)
+        copy((KL, 0, 12), ("ki" + s, 0, 12))
+        for x in range(2):
+            gath((ML, CW * x, CW * x + CW), ("DM", 0, 16), (KL, 6 * x, 6 * x + 6), (LV, 0, CW), A.mult)
+        mm((PK, 384, 396), [(sel("S1", u), (ML, u, M, 16)) for u in range(16)])
+        copy((KL, 12, 24), (PK, 384, 396))
+        gath(("EDU" + s, 0, M), RT, (KL, 12, 24))
+        copy(("EV" + s, 0, M), ("EDU" + s, 0, M))
+        mm((PK, 400, 496), [(BOH, (ML, 0, CW))])
+        copy(("LR",) + j, (PK, 400, 496))
+        gath(("NCB",) + j, RT, (KL, 12, 18), ("NM", j[0] + t, j[1] + t), A.mult)
+
+    def farthest(t, c):
+        s, j = str(c), (CW * c, CW * c + CW)
+        PK, MT = "PK" + s, "MT" + s
+        gath(("KEEP",) + j, ("MN" + s, CW, M), ("BC", 0, 6), ("NK",) + j, A.is_lt)
+        tt((PK, 0, CW), (PK, 0, CW), ("KEEP",) + j, A.mult)
+        scan((MT, M, M + CW), ("NDZ", 0, CW), (PK, 0, CW), -B25, A.add, A.max)
+        tt(("C2", 16, 15 + CW), (MT, M, M + CW - 1), (PK, 1, CW), A.min)
+        scan((MT, M + CW, 2 * M), ("NDZ", 0, CW), ("C2", 15, 15 + CW), -B25, A.add, A.max)
 
     def entries(t, c):
         s = str(c)
         for k in range(2):
-            for q in awayabs(("AD" + s, NP * k), ("DAB" + s, NP * k), "ZT" + s):
-                d = (NP * k + 512 * q, NP * k + 512 * q + 512)
-                (sgath if 6 * c + 3 * k + q in BYS else gath)(("DAB" + s,) + d, ("X", 0, W), ("EDU" + s, d[0] // 16, d[1] // 16))
-            o = CW + CW * k
-            mm(("PC" + s, o, o + CW), [(SELS[u], ("AD" + s, NP * k + u, NP * k + NP, 16)) for u in range(16)] + [(IDB, ("P2C", CW * k, CW * k + CW))])
-
-    def farthest(t, c):
-        j, w = (CW * c, CW * c + CW), (M * c, M * c + M)
-        PC, FK, FH = "PC%d" % c, ("FK",) + j, ("FH", 16 * c, 16 * c + 12)
-        BA, BB = ("BA", 0, 6), ("BA", 6, 12)
-        gath(("KEEP",) + j, ("MN", w[0] + CW, w[1]), ("BC", 0, 6), ("NK",) + j, A.is_lt)
-        tt(FK, ("PD%d" % c, 0, CW), ("KEEP",) + j, A.mult)
-        scan((PC, 288, 384), ("NDZ", 0, CW), FK, -B22, A.add, A.max)
-        tt(("C2", 16, 15 + CW), (PC, 288, 383), ("FK", j[0] + 1, j[1]), A.min)
-        scan((PC, 384, 480), ("NDZ", 0, CW), ("C2", 15, 15 + CW), -B22, A.add, A.max)
-        copy(FH, (PC, 303, 480, 16))
-        gath(("KEEP",) + j, FH, BB, FK, A.is_gt)
-        tt(("LK",) + j, ("KEEP",) + j, ("LF",) + j, A.mult)
-        gath(("P12", w[0], w[0] + CW), FH, BA, FK, A.is_equal)
-        gath(("P12", w[0] + CW, w[1]), FH, BB, FK, A.is_equal)
+            for q in awayabs("AD" + s, "DAB" + s, "LV" + s, NP * k):
+                d = (NP * k + XW * q, NP * k + XW * q + XW)
+                (gath if NP // XW * (2 * c + k) + q in BYV else sgath)(("DAB" + s,) + d, ("X", 0, W), ("EDU" + s, d[0] // 16, d[1] // 16))
+            o = M + CW * k
+            mm(("PK" + s, o, o + CW), [(IDB, ("P2H", CW * k, CW * k + CW)), (IDB, ("P2L", 0, CW))]
+               + [(sel("SK", u), ("AD" + s, NP * k, NP * k + NP, u)) for u in range(16)])
 
     def tail(t, c):
-        s, j, w, k = str(c), (CW * c, CW * c + CW), (M * c, M * c + M), (12 * c, 12 * c + 12)
-        PD, PC = "PD" + s, "PC" + s
-        MG, nx = "MG%d%d" % (t, c), "LN%d%d" % (t + 1, c)
-        scan(("MN",) + w, ("DZ", 0, M), (PC, CW, 3 * CW), B22, A.add, A.min)
-        ts(("ki",) + k, ("MN", w[0] + 15, w[1], 16), 255, A.bitwise_and)
-        ts(("JP",) + k, ("ki",) + k, 16.0, A.mult, PU, A.add)
-        (sgath if c in SD_ else gath)(("dab",) + w, ("DAB" + s, 0, 2 * NP), ("JP",) + k)
-        copy(("JL",) + k, ("ki",) + k)
-        xa, xb = ("dab", w[0], w[0] + CW), ("dab", w[0] + CW, w[1])
-        mm((PC, 0, CW), [(IDB, xa), (NIDB, xb)])
-        mm((PD, CW, 2 * CW), [(IDB, xa), (IDB, xb)])
-        act(("DA",) + j, (PC, 0, CW), F.Abs)
-        mm((PC, 480, 486), [(SELS[u], ("DA", j[0] + u, j[1], 16)) for u in range(16)])
-        gath(("GM",) + w, ("EDF" + s, 0, M), ("JL",) + k, ("DM", 0, M), A.mult)
-        scan(("SE",) + w, ("MS", 0, M), ("GM",) + w, 0.0, A.mult, A.add)
-        gath(("PE2",) + w, ("SE",) + w, ("BC", 0, 12), ("P12",) + w, A.mult)
-        new = [(IDH, ("LK",) + j), (IDH, ("PE2", w[0], w[0] + CW)), (IDH, ("PE2", w[0] + CW, w[1]))]
-        mm((PD, 192, 288), new)
-        tt(("EL",) + j, ("EDF" + s, CW, M), (PD, 192, 288), A.subtract)
-        act(("EL", j[0], j[1], 16), ("EL", j[0], j[1], 16), F.Copy, 0.0)
-        AC, k = ("ACA", 8 * c, 8 * c + 6), (6 * c, 6 * c + 6)
-        ts(AC, (PC, 480, 486), ("THN", t, t + 1), A.is_lt)
-        gath(("EAC",) + j, AC, ("BA", 0, 6), ("EL",) + j, A.mult)
-        mm((PD, 192, 288), new + [(IDH, ("EAC",) + j)])
-        if t < TV - 1:
-            ts((MG, CW, 2 * CW), (PD, CW, 2 * CW), 0.5, A.mult, -0.25, A.add)
-            copy((MG, 2 * CW, MW), AC)
-            ts((MG, 0, CW), (PD, 192, 288), -1.0, A.add)
-            send(1, (MG, 0, MW), (nx, 0, MW), "ar%d%d" % (t + 1, c))
+        s, j = str(c), (CW * c, CW * c + CW)
+        PK, PT, MT, JP, L, dab, Q = "PK" + s, "PT" + s, "MT" + s, "JP" + s, ("LV" + s, 0, CW), "dab" + s, "Q" + s
+        scan((MT, 0, M), ("DZ", 0, M), (PK, M, 2 * M), B25, A.add, A.min)
+        ts(("kj" + s, 0, 24), (MT, 15, 2 * M, 16), 4095, A.bitwise_and)
+        copy((JP, 0, 24), ("kj" + s, 0, 24))
+        xa, xb = (dab, 0, CW), (dab, CW, M)
+        if c in MX_:
+            gath(("DA",) + j, ("DAB" + s, 0, 2 * NP), (JP, 0, 6))
+            gath(xa, ("DAB" + s, 0, 2 * NP), (JP, 6, 12), ("DA",) + j, A.max)
+            gath(xb, ("DAB" + s, 0, 2 * NP), (JP, 6, 12), ("DA",) + j, A.min)
+            mm((PK, CW, M), [(BO, xa), (("NBO", 0, 128), xb)])
         else:
-            ts(("ZU",) + j, (PD, CW, 2 * CW), 0.5, A.mult, -0.25, A.add)
+            (sgath if c in SD_ else gath)((dab, 0, M), ("DAB" + s, 0, 2 * NP), (JP, 0, 12))
+            mm((PK, CW, M), [(IDB, xa), (NIDB, xb)])
+            act(("DA",) + j, (PK, CW, M), F.Abs)
+            mm((PK, CW, M), [(BO, ("DA",) + j)])
+        ts(("SG",) + j, (PK, CW, M), ("THN", t, t + 1) if t else ("TH", 0, 1), A.is_lt)
+        mm((PK, 496, 502), [(sel("SH", u), ("SG", j[0] + u, j[1], 16)) for u in range(16)])
+        gath(("ME" + s, 0, M), ("DMB", 0, 2 * NP), (JP, 0, 12), ("EV" + s, 0, M), A.mult)
+        (sgath if c in SP_ else gath)(("P12" + s, 0, M), ("DMR", 0, 16), (JP, 12, 24))
+        if t < TV - 1:
+            mm((PT, 192 + CW, 416), [((dab, 0, 128), HB), ((dab, CW, MW), HB)])
+        else:
+            mm((PT, 192 + CW, 192 + M), [(HB, xa), (HB, xb)])
+        mm((PT, 0, M), [(BOH, ("ME" + s, 0, M)), (NIDH, L, 128, (PT, 0, CW)), (NIDH, L, 128, (PT, CW, M))])
+        tt((Q, 0, M), (PT, 0, M), ("P12" + s, 0, M), A.mult)
+        Qa, Qb, Eb = (Q, 0, CW), (Q, CW, M), ("EV" + s, CW, M)
+        mm((PT, 0, CW), [(HP, Eb), (HN, L), (HN, Qa), (HN, Qb)])
+        tt(("EAC" + s, 0, CW), (PT, 0, CW), ("SG",) + j, A.mult)
+        mm((PT, 192, 192 + CW), [(IDH, L), (IDH, Qa), (IDH, Qb), (IDH, ("EAC" + s, 0, CW))])
+        if t < TV - 1:
+            MG = ("MG%d%d" % (t, c), 0, MW)
+            ts(MG, (PT, 192, 416), -0.25, A.add)
+            send(1, MG, ("LN%d%d" % (t + 1, c), 0, MW), "ar%d%d" % (t + 1, c))
+        else:
+            ts(("ZU",) + j, (PT, 192 + CW, 192 + M), -0.25, A.add)
             copy(("yzo",) + j, ("ZU",) + j)
-            ts(("LK",) + j, (PD, 192, 288), -1.0, A.add)
-            turn("ET" + s, ("LK",) + j)
-            a2d(6 * c, "ET" + s, 3)
-            copy4(("ylo",) + j, 6 * c, 6 * c + 3)
-        e = ("SG" + s, 15, CW, 16)
-        tt(("LAM",) + k, e, AC, A.mult)
-        tt(("LMC",) + k, e, ("CJ",) + k, A.subtract)
-        tt(("LMC",) + k, ("LMC",) + k, AC, A.mult)
-        tt(("NCB",) + j, ("EA" + s, 0, CW), ("NM", j[0] + t, j[1] + t), A.mult)
+            act(("ylo",) + j, (PT, 192, 192 + CW))
+
+    def writes(t):
+        mm((PU, 208, 400), [(R0, ("LV0", 0, CW), 128, (PU, 208, 208 + CW))])
+        mm((PU, 208, 400), [(R0, ("LV1", 0, CW), 128, (PU, 208 + CW, 400))])
+        if t == 0:
+            act(("L0R0", 0, M), (PU, 208, 400))
+            for k in range(1, N):
+                send(k, ("L0R0", 0, M), ("L0R%d" % k, 0, M), "al%d" % k)
+        tt(("M2", 0, M), (PU, 208, 400), ("DM", t, t + M), A.mult)
 
     def update(t):
-        copy(("LAMU", 0, 12), ("LAM", 0, 12))
-        gath(("LR", 0, M), ("IW", 0, 2056), ("LAMU", 0, 12))
-        at, pos = [], 0
+        mm((PU, 0, M), [(IDH, ("LR", 0, M)), (IDB, ("C4K", 0, M))], last=False)
+        pos = 0
         for v in range(12):
-            n = M - 16 * v
-            ts(("EW", pos, pos + n), ("LR", 16 * v, M), ("LAM", v, v + 1), A.is_equal)
-            at.append(pos)
-            pos += n
-        fns, B = [], "PD1"
-
-        def one(l, lo, hi, p, st, sp):
-            return lambda: g.tensor.matmul(T[B][:, 288 + lo:288 + hi], sl((l, 0, 128)), sl(("EW", p, p + hi - lo)), st, sp)
-        fns.append(one("LTR", 0, M, 0, True, False))
-        fns.append(one("UTR", 16, M, 16, False, False))
-        for v in range(1, 12):
-            fns.append(one("LTR", 16 * v, 16 * v + 16, at[v], False, v == 11))
+            n, c = M - 16 * v, v // 6
+            if v % 6 == 0:
+                j = (CW * c, CW * c + CW)
+                mm((PU,) + j, [(("N4K", 0, 128), ("SG",) + j)], first=False, last=False)
+            ts(("EW", pos, pos + n), ("LR", 16 * v, M), ("PK%d" % c, 384 + v % 6, 385 + v % 6), A.is_equal, ("PK%d" % c, 496 + v % 6, 497 + v % 6), A.mult)
+            terms = [(("LTR", 0, 128), ("EW", pos, pos + 16), 128, (PU, 16 * v, 16 * v + 16))]
             if v < 11:
-                fns.append(one("BO", 16 * v + 16, M, at[v] + 16, False, False))
-        op("P", fns, [("EW", 0, 1248), ("LTR", 0, 128), ("UTR", 0, 128), ("BO", 0, 128)], [(B, 288, 480)], 0.03 + 2200 * PEC)
-        tt(("DL", 0, M), (B, 288, 480), ("DM", 0, M), A.mult)
-        scan(("SD", 0, M), ("MS", 0, M), ("DL", 0, M), 0.0, A.mult, A.add)
-        W2 = ("W2", 0, 12)
-        ts(W2, ("SD", 15, M, 16), 0.5, A.is_lt)
-        tt(W2, W2, ("LMC", 0, 12), A.mult)
-        tt(W2, W2, ("CI", 0, 12), A.add)
-        copy(("WLU", 0, 12), W2)
+                terms.append((("BO4", 0, 128), ("EW", pos + 16, pos + n), 128, (PU, 16 * v + 16, M)))
+            mm((PU, 0, M), terms, first=False, last=v == 11)
+            pos += n
+        tt(("WM", 0, M), (PU, 0, M), ("CIM", 0, M), A.min)
+        mm((PU, 192, 204), [(sel("S1", u), ("WM", u, M, 16)) for u in range(16)])
+        copy(("WLU", 0, 12), (PU, 192, 204))
         op("V", [lambda: g.vector.tensor_tensor(T.R[:].indirect(sl(("WLU", 0, 12))), sl(("NCB", 0, M)), sl(("M2", 0, M)), A.add)],
-           [("WLU", 0, 12), ("NCB", 0, M), ("M2", 0, M)], [("R", 0, W + M)], 0.05 + M * 3.5 * CYC)
+           [("WLU", 0, 12), ("NCB", 0, M), ("M2", 0, M)], [("R", 0, RW)], 0.05 + M * 3.5 * CYC)
 
     def count(t):
+        def add(c):
+            return lambda: g.scalar.activation(sl(("ACO", 0, 6)), sl(("PK%d" % c, 496, 502)), F.Copy, accum_out=sl(("CNT", c, c + 1)))
         for c in range(2):
-            copy(("AC2", 6 * c, 6 * c + 6), ("LN%d%d" % (t, c), 2 * CW, MW))
-        mm(("PC0", 488, 500), [(("ONE", 0, 128), ("AC2", 0, 12))])
-        act(("nn", 0, 12), ("PC0", 488, 500), F.Copy, acc=("ns", 0, 1))
-        copy(("ni", 0, 1), ("ns", 0, 1))
-        ts(("ni", 0, 1), ("ni", 0, 1), 63, A.bitwise_and)
-        ts(("THN", t, t + 1), ("ni", 0, 1), 256.0, A.mult, ("TH", 0, 1), A.add)
+            op("S", [add(c)], [("PK%d" % c, 496, 502)], [("ACO", 0, 6), ("CNT", c, c + 1)], 0.13)
+        mm((PU, 420, 421), [(("ONE", 0, 128), ("CNT", 0, 1)), (("ONE", 0, 128), ("CNT", 1, 2))], slow=4)
+        copy(("ni", 0, 1), (PU, 420, 421))
+        ts(("NS%d" % t, 0, 1), ("ni", 0, 1), 63, A.bitwise_and)
+        send(1, ("NS%d" % t, 0, 1), ("NL%d" % (t + 1), 0, 1), "an%d" % (t + 1))
 
-    l0x(0)
     for t in range(TV):
-        bonus[0] = 0
-        stage1(t, 0)
+        if t == 0:
+            writes(t)
         bonus[0] = 1
-        tt(("M2", 0, M), ("DM", t, t + M), ("L0R%d" % (t % 4), 0, M), A.mult)
-        stage1(t, 1)
-        bonus[0] = 4
-        if t > 0:
-            count(t)
+        stage1(t, 0)
         bonus[0] = 2
-        farthest(t, 0)
-        entries(t, 0)
+        stage1(t, 1)
         bonus[0] = 3
-        farthest(t, 1)
-        entries(t, 1)
-        bonus[0] = 4
+        if t == 0:
+            copy(("R", 0, 1024), ("Ri", 0, 1024))
+            copy(("R", 1024, 2048), ("Ri", 1024, 2048))
+        else:
+            writes(t)
+            ts(("THN", t, t + 1), ("NL%d" % t, 0, 1), ("TH", 0, 1), A.add)
         if t < 3:
-            l0x(t + 1)
+            spread(t + 1)
+        bonus[0] = 4
+        farthest(t, 0)
+        bonus[0] = 5
+        entries(t, 0)
+        bonus[0] = 4
+        farthest(t, 1)
+        bonus[0] = 6
+        entries(t, 1)
         bonus[0] = 7
         tail(t, 0)
-        bonus[0] = 6
+        bonus[0] = 8
         tail(t, 1)
-        bonus[0] = 5
+        bonus[0] = 9
         update(t)
-        bonus[0] = 6
+        bonus[0] = 10
+        if t < TV - 1:
+            count(t)
+    bonus[0] = 0
+    mm(("XD0", 0, 256), [(("IDF", 0, 128), ("R", 1536, 1792)), (("IDF", 0, 128), ("R", 1792, 2048))], slow=4, last=False)
     for h in range(3):
         copy(("RH", 512 * h, 512 * h + 512), ("R", 512 * h, 512 * h + 512))
-    for h in range(4):
-        blocks = [("R", 1536, 1792), ("R", 1792, 2048)] if h == 0 else [("RH", 512 * h - 512, 512 * h - 256), ("RH", 512 * h - 256, 512 * h)]
-
-        def part(h, blocks):
-            return lambda k: g.tensor.matmul(T.XD0[:, 0:256], sl(("IDF" if h == 0 else "IDH", 0, 128)), sl(blocks[k]), h == 0 and k == 0, h == 3 and k == 1)
-
-        def call(f, k):
-            return lambda: f(k)
-        op("P", [call(part(h, blocks), k) for k in range(2)], [rg(b) for b in blocks] + [("IDF", 0, 128), IDH], [("XD0", 0, 256)], 2 * 256 * PEC * (4 if h == 0 else 1))
+        mm(("XD0", 0, 256), [(IDH, ("RH", 512 * h, 512 * h + 256)), (IDH, ("RH", 512 * h + 256, 512 * h + 512))], first=False, last=h == 2)
     act(("yro", 0, 256), ("XD0", 0, 256))
     store(T.yz, ("yzo", 0, M))
     store(T.yl, ("ylo", 0, M))
@@ -577,7 +601,7 @@ def rank_program(g, core, T, topo):
             done[i], last[s] = (s, v, {s: v}), v
             continue
         kn = know[e]
-        for j in sorted(o["d"], key=lambda j: -ops[j]["s"]):
+        for j in sorted(o["d"] - o["free"], key=lambda j: -ops[j]["s"]):
             s, v, clk = done[j]
             if kn.get(s, 0) < v:
                 queue[e].wait_ge(T.sem[s], v)

from concourse.mybir import AluOpType, ActivationFunctionType

A = AluOpType
F = ActivationFunctionType
N, W, M, TV = 4, 2048, 192, 6
CW, NP = 96, 1536
MW = CW + 128
RW = W + 2 * M
K12, B25 = 4096.0, float(2 ** 25)
XW, XN = 768, 2
PU = "PT0"
XV = ()
BYV = (0, 2, 4, 6)
SD_ = (0, 1)
SP_ = ()
MX_ = (0,)
LV0 = (3, 4, 5)
BQ = 6
CUT = 6
TWICE = (1,)
CF_ = (1,)

SCRATCH = {
    "X": ("sbuf", [128, W], "bfloat16"), "Ri": ("sbuf", [128, W], "int32"), "R": ("sbuf", [128, RW], "float32"), "RH": ("sbuf", [128, W], "float16"),
    "l0i": ("sbuf", [128, M], "int32"), "thi": ("sbuf", [8, 1], "int32"), "thf": ("sbuf", [8, 1], "float32"), "G8": ("sbuf", [8, 128], "float32"),
    "ylo": ("sbuf", [128, M], "float32"), "yro": ("sbuf", [128, 256], "float32"), "DMB": ("sbuf", [128, 2 * NP], "bfloat16"),
}
PLACE, DTY, END = {}, {}, {}


def piece(buf, dtype, width, *names):
    for name in names:
        PLACE[name] = (buf, END.get(buf, 0))
        DTY[name] = dtype
        END[buf] = END.get(buf, 0) + (width + 15) // 16 * 16
        SCRATCH[buf] = ("sbuf", [128, END[buf]], dtype)


piece("AI", "int32", 24, "IPi", "ci", "BCi", "ni", "ki0", "ki1", "kj0", "kj1")
piece("AI", "int32", 16, *["NS%d" % t for t in range(TV - 1)])
piece("AI", "int32", 16, *["NL%d" % t for t in range(1, TV)])
piece("AF", "float32", 2 * NP, "LX0", "LX1", "LX2", "LX3")
piece("AF", "float32", 208, "IC", "I15", "DM", "NM", "IG")
piece("AF", "float32", M, "L0R0", "L0R1", "L0R2", "L0R3", "M2", "NCB", "tmp", "DZ", "NDZ", "NK", "KEEP", "CIM", "DS", "IDF", "ONE")
piece("AF", "float32", 16 + CW, "C1", "C2")
piece("AF", "float32", CW, "CC")
piece("AF", "float32", 24, "cf", "DMR", "TH", "THN", "CNT")
piece("AH", "float16", NP, "SIH")
piece("AH", "float16", 144, "S1")
piece("AH", "float16", 128, "IDH", "NIDH", "BOH", "R0", "HP", "HN", "L0T0", "L0T1")
piece("AH", "float16", M, "LR", "WM")
piece("AU", "uint16", 24, "BC", "WLU")
piece("AU", "uint16", MW, *["LN%d%d" % (k, c) for k in range(TV) for c in range(2)])
piece("AU", "uint16", MW, *["MG%d%d" % (k, c) for k in range(TV - 1) for c in range(2)])
piece("AU", "uint16", M, "ZU")
piece("AB", "bfloat16", 128, "IDB", "NIDB", "HB", "N4K", "BO", "NBO", "BO4", "LTR", "UTR")
piece("AB", "bfloat16", 144, "SK", "SC", "SH")
piece("AB", "bfloat16", NP, "IX")
piece("AB", "bfloat16", M, "PDC", "PCC", "PCD", "P2H", "P2L", "zin", "yzo", "DA", "SG", "C4K")
piece("AB", "bfloat16", 16, "ACO")
piece("AB", "bfloat16", 1248, "EW")
for c_ in "01":
    piece("AI", "int32", M, "MN" + c_)
    piece("AI", "int32", 2 * M, "MT" + c_)
    piece("AH", "float16", MW, "LV" + c_)
    piece("AH", "float16", M, "ML" + c_, "EV" + c_, "ME" + c_, "Q" + c_, "EAC" + c_)
    piece("AU", "uint16", 24, "KL" + c_, "JP" + c_)
    piece("AU", "uint16", M, "EDU" + c_)
    piece("AB", "bfloat16", MW, "dab" + c_)
    piece("AB", "bfloat16", M, "P12" + c_)
    piece("AB", "bfloat16", NP, "XG" + c_)
    piece("AB", "bfloat16", 2 * NP, "DAB" + c_)
    SCRATCH["AX" + c_] = ("sbuf", [128, 6, 256], "bfloat16")
    SCRATCH["EQ" + c_] = ("sbuf", [128, 6, 256], "bfloat16")
    SCRATCH["AD" + c_] = ("sbuf", [128, 12, 256], "bfloat16")
for n_ in ("PK0", "PK1", "PT0", "PT1", PU):
    SCRATCH[n_] = ("psum", [128, 512], "float32")
for n_ in range(XN):
    SCRATCH["XD%d" % n_] = ("psum", [128, (XW + 511) // 512 * 512], "float32")
LOADS = ["l0", "z0", "th", "ex0", "ex1", "xt", "mb"]
SEMAPHORES = (["sV", "sS", "sP", "sG", "snt", "st"] + ["ld_" + k for k in LOADS] + ["ar%d%d" % (t, c) for t in range(1, TV) for c in range(2)]
              + ["al" + k for k in "123"] + ["an%d" % t for t in range(1, TV)])

CYC, OVH, WAKE, SAME, NET = 0.00083 * 1.25, 0.03, 0.1, 0.06, 3.5
GATH, PEC = 1.55, 0.0005


def is_psum(b):
    return b in SCRATCH and SCRATCH[b][0] == "psum"


def build(ops):
    acc, pe = {}, {}
    for i, o in enumerate(ops):
        deps = set()
        for wr, lst in ((0, o["r"]), (1, o["w"])):
            for b, lo, hi in lst:
                for (j, l2, h2, w2) in acc.get(b, ()):
                    over = l2 < hi and lo < h2
                    if o.get("apart") and ops[j].get("apart") == o["apart"]:
                        continue
                    if (over and (wr or w2)) or (is_psum(b) and ops[j]["e"] != o["e"]):
                        deps.add(j)
        for wr, lst in ((0, o["r"]), (1, o["w"])):
            for b, lo, hi in lst:
                old = acc.setdefault(b, [])
                if wr and not is_psum(b) and not o.get("apart"):
                    old[:] = [x for x in old if not (lo <= x[1] and x[2] <= hi)]
                if is_psum(b) and o["e"] == "P":
                    old[:] = []
                old.append((i, lo, hi, wr))
        if "after" in o:
            deps.add(o["after"])
        o["free"] = set()
        if o["e"] == "P":
            b = o["w"][0][0]
            if b in pe and pe[b] not in deps:
                o["free"].add(pe[b])
                deps.add(pe[b])
            if o.get("adds"):
                o["free"] |= set(j for j in deps if ops[j]["e"] == "P")
            pe[b] = i
        o["d"] = deps
    return ops


TICK, HOLD, LAM, ROUNDS = 0.05, 0.0, 2.0, 10
BON = [0.0] * 9 + [-10.0, 0.0, 0.0]


def lag(ops, j, i):
    return WAKE if ops[j]["e"] != ops[i]["e"] else 0.0 if j in ops[i]["free"] or i in ops[j]["free"] else SAME


def place(ops, order, before, back):
    busy, start, fin = {}, {}, {}
    for i in order:
        o = ops[i]
        lat = o.get("lat", 0.0)
        s = max([fin[j] + lag(ops, j, i) for j in before[i]] + [0.0]) + (lat if back else 0.0)
        if o["e"] != "net":
            line = busy.setdefault(o["e"], [])
            k = len(line)
            while k and line[k - 1][1] > s:
                k -= 1
            while k < len(line) and line[k][0] < s + o["t"] - 1e-9:
                s = max(s, line[k][1])
                k += 1
            line.insert(k, (s, s + o["t"]))
        start[i], fin[i] = s, s + o["t"] + (0.0 if back else lat)
    return start, fin


def schedule(ops):
    n = len(ops)
    left = [len(o["d"]) for o in ops]
    users = [[] for _ in ops]
    for i, o in enumerate(ops):
        for j in o["d"]:
            users[j].append(i)
    tail = [0.0] * n
    for i in range(n - 1, -1, -1):
        tail[i] = ops[i]["t"] + ops[i].get("lat", 0.0) + max([tail[j] + lag(ops, i, j) for j in users[i]] + [0.0])
    for i in range(n):
        tail[i] += BON[ops[i]["bi"]]
    free, fin, at = {}, [0.0] * n, [0.0] * n
    ready = [i for i in range(n) if left[i] == 0]
    est = {i: 0.0 for i in ready}
    while ready:
        start = {i: max(est[i], free.get(ops[i]["e"], 0.0)) if ops[i]["e"] != "net" else est[i] for i in ready}
        f = min(ready, key=lambda i: (start[i] + HOLD * ops[i]["t"], i))
        i = min([i for i in ready if ops[i]["e"] == ops[f]["e"] and start[i] <= start[f] + HOLD * ops[f]["t"] + TICK],
                key=lambda i: (LAM * (start[i] - start[f]) - tail[i], i))
        ready.remove(i)
        at[i], fin[i] = start[i], start[i] + ops[i]["t"] + ops[i].get("lat", 0.0)
        free[ops[i]["e"]] = start[i] + ops[i]["t"]
        for j in users[i]:
            left[j] -= 1
            est[j] = max(est.get(j, 0.0), fin[i] + lag(ops, i, j))
            if left[j] == 0:
                ready.append(j)
    best = (max(fin), at)
    for _ in range(ROUNDS):
        _, late = place(ops, sorted(range(n), key=lambda i: (-fin[i], -i)), users, True)
        at, fin = place(ops, sorted(range(n), key=lambda i: (-late[i], i)), [o["d"] for o in ops], False)
        if max(fin.values()) < best[0]:
            best = (max(fin.values()), at)
    for i in range(n):
        ops[i]["s"] = best[1][i]
    return sorted(range(n), key=lambda i: (ops[i]["s"], i)), best[0]


def program(g, core, T, topo):
    ops = []
    rank = T.rank_of(core)
    bonus = [0]

    def op(e, fns, r, w, t, **k):
        o = {"e": e, "f": fns, "r": r, "w": w, "t": t, "bi": bonus[0]}
        o.update(k)
        ops.append(o)

    def sl(x, p=128):
        if x[0] in SCRATCH and len(SCRATCH[x[0]][1]) == 3:
            if len(x) == 3 and x[2] - x[1] == 256:
                return T[x[0]][0:p, x[1] // 256, :]
            if len(x) == 3:
                return T[x[0]][0:p, x[1] // 256:x[2] // 256, :]
            return T[x[0]][0:p, x[1] // 256:x[2] // 256, 16 * x[3]:16 * x[3] + 16]
        b, o = PLACE.get(x[0], (x[0], 0))
        return T[b][0:p, o + x[1]:o + x[2]] if len(x) == 3 else T[b][0:p, o + x[1]:o + x[2]:x[3]]

    def rg(x):
        return (x[0], x[1], x[2])

    def num(x):
        return len(range(*x[1:]))

    def two(x):
        return (DTY[x[0]] if x[0] in DTY else SCRATCH[x[0]][2]) in ("bfloat16", "float16", "uint16")

    def cyc(c):
        return OVH + max(c, 64) * CYC

    def copy(o, i, p=128):
        op("V", [lambda: g.vector.tensor_copy(sl(o, p), sl(i, p))], [rg(i)], [rg(o)], cyc(num(o) * (0.5 if two(o) and two(i) else 1)))

    def tt(o, a, b, f):
        op("V", [lambda: g.vector.tensor_tensor(sl(o), sl(a), sl(b), f)], [rg(a), rg(b)], [rg(o)], cyc(num(o) * (1 if is_psum(a[0]) or is_psum(b[0]) else 2)))

    def ts(o, a, s1, f1, s2=None, f2=None):
        def run():
            p, q = [sl(x) if isinstance(x, tuple) else x for x in (s1, s2)]
            if f2 is None:
                return g.vector.tensor_scalar(sl(o), sl(a), p, None, f1)
            return g.vector.tensor_scalar(sl(o), sl(a), p, q, f1, f2)
        op("V", [run], [rg(a)] + [rg(x) for x in (s1, s2) if isinstance(x, tuple)], [rg(o)], cyc(num(o) * (0.5 if two(o) and two(a) else 1)))

    def scan(o, d0, d1, ini, f0, f1):
        op("V", [lambda: g.vector.tensor_tensor_scan(sl(o), sl(d0), sl(d1), ini, f0, f1)], [rg(d0), rg(d1)], [rg(o)], cyc(num(o)))

    def fill(o, v):
        op("V", [lambda: g.vector.memset(sl(o), v)], [], [rg(o)], cyc(num(o) * (0.5 if two(o) else 1)))

    def gath(o, w, off, other=None, f=None):
        def run():
            x = sl(w).indirect(sl(off))
            return g.vector.tensor_copy(sl(o), x) if other is None else g.vector.tensor_tensor(sl(o), x, sl(other), f)
        op("V", [run], [rg(w), rg(off)] + ([rg(other)] if other else []), [rg(o)], 0.05 + num(o) * GATH * CYC)

    def act(o, i, f=F.Copy, scale=1.0, p=128, bias=0.0):
        op("S", [lambda: g.scalar.activation(sl(o, p), sl(i, p), f, bias, scale)], [rg(i)], [rg(o)], 0.1 + num(o) * CYC)

    def sgath(o, w, off):
        op("S", [lambda: g.scalar.activation(sl(o), sl(w).indirect(sl(off)), F.Copy)], [rg(w), rg(off)], [rg(o)], 0.07 + num(o) * GATH * CYC)

    def mm(o, terms, p=128, slow=1, first=True, last=True):
        def mk(k, x):
            q = x[2] if len(x) > 2 else 128
            y = x[3] if len(x) > 3 else o
            return lambda: g.tensor.matmul(sl(y, p), sl(x[0], q), sl(x[1], q), first and k == 0, last and k == len(terms) - 1)
        step = 1 if num(o) > 256 else CUT
        for k in range(0, len(terms), step):
            part = terms[k:k + step]
            op("P", [mk(k + n, x) for n, x in enumerate(part)], [rg(y) for x in part for y in x[:2]], [rg(o)],
               slow * PEC * sum(max(num(x[3] if len(x) > 3 else o), 64) for x in part), adds=k > 0 or not first)

    def load(out, i, sem, b, n, lo=0):
        op("Y", [lambda: g.sync.dma_start(out, i)], [], [(b, lo, lo + n)], 0.1, lat=2.5 + n / 1000.0, sem=("ld_" + sem, 16))

    def store(out, x):
        op("Y", [lambda: g.sync.dma_start(out[:], sl(x))], [rg(x)], [], 0.1, lat=2.0, sem=("st", 16))

    def iota(x, pat, base, cm, fl=False):
        op("G", [lambda: g.iota(sl(x), pat, base, cm, allow_small_or_imprecise_dtypes=True) if fl else g.iota(sl(x), pat, base, cm)], [], [rg(x)], 0.13 + num(x) * 2 * CYC)

    def send(k, x, y, sem):
        src, d = T.cores[(rank - k) % N], T.cores[(rank + k) % N]
        rid, pid = topo.addr(d, core)
        m = topo.mask(core, d)
        op("G", [lambda: g.remote_dma(sl(y), sl(x), T.sem[sem], T.sem.snt, pid, rid, m)], [rg(x)], [], 0.6, send=len(topo.engines(core, d)))
        op("net", [], [], [rg(y)], NET, sem=(sem, len(topo.engines(src, core))), after=len(ops) - 1)

    def sel(name, u):
        return (name, 15 - u, 143 - u)

    xd = [0]

    def bank():
        xd[0] = (xd[0] + 1) % XN
        return "XD%d" % xd[0]

    load(T.l0i[:], T.l0[:], "l0", "l0i", M)
    load(T.X[:], T.xt[:], "xt", "X", W)
    load(sl(("zin", 0, M)), T.z0[:], "z0", "zin", M)
    load(T.Ri[:, 0:1024], T.ex[:, 0:1024], "ex0", "Ri", 1024)
    load(T.Ri[:, 1024:2048], T.ex[:, 1024:2048], "ex1", "Ri", 1024, 1024)
    load(T.thi[:], T.th[:], "th", "thi", 1)
    iota(("IPi", 0, 1), [[0, 1]], 0, 1)
    iota(("IC", 0, 144), [[1, 144]], 0, 0, True)
    iota(("IG", 0, M), [[1, 12], [0, 16]], 0, 0, True)
    for q in range(3):
        iota(("IX", 512 * q, 512 * q + 512), [[1, 32], [0, 16]], 32 * q, 0, True)
    iota(("I15", 0, 208), [[0, 13], [1, 16]], 0, 0, True)
    iota(("BCi", 0, 6), [[16, 6]], 15, 0)
    iota(("CIM", 0, M), [[2, M]], W, 0, True)
    PP, PG0, PG, PZ, NZ, PE, PR, P16 = [("cf", k, k + 1) for k in range(8)]
    ts(("ci", 0, 1), ("IPi", 0, 1), 15, A.bitwise_and)
    ts(("ci", 1, 2), ("IPi", 0, 1), 4, A.arith_shift_right)
    copy(PP, ("IPi", 0, 1))
    copy(("cf", 1, 3), ("ci", 0, 2))
    IC1, I15, tmp = ("IC", 0, 128), ("I15", 0, M), ("tmp", 0, CW)
    IDB, NIDB, IDH, NIDH, HB, BO, BOH, R0, HP, HN = [(k, 0, 128) for k in ("IDB", "NIDB", "IDH", "NIDH", "HB", "BO", "BOH", "R0", "HP", "HN")]
    ts(PZ, PG0, 0.0, A.is_equal)
    ts(NZ, PG0, 0.0, A.is_gt)
    ts(PE, PG, 16.0, A.mult, 15.0, A.add)
    ts(PR, PG0, -1.0, A.mult, 16.0, A.add)
    ts(P16, PG0, 16.0, A.mult)
    ts(IDB, IC1, PP, A.is_equal)
    act(NIDB, IDB, F.Copy, -1.0)
    act(HB, IDB, F.Copy, 0.5)
    act(("N4K", 0, 128), IDB, F.Copy, -K12)
    act(("IDF", 0, 128), IDB)
    copy(IDH, IDB)
    ts(NIDH, IDB, -1.0, A.mult)
    ts(HP, IDB, NZ, A.mult)
    ts(HN, HP, -1.0, A.mult)
    ts(BO, ("IG", 0, 128), PG, A.is_equal)
    copy(BOH, BO)
    ts(R0, BO, PZ, A.mult)
    act(("BO4", 0, 128), BO, F.Copy, K12)
    act(("NBO", 0, 128), BO, F.Copy, -1.0)
    ts(("UTR", 0, 128), IC1, PP, A.is_gt)
    tt(("LTR", 0, 128), ("UTR", 0, 128), ("BO4", 0, 128), A.mult)
    for q in range(3):
        ts(("SIH", 512 * q, 512 * q + 512), ("IX", 512 * q, 512 * q + 512), PP, A.is_equal)
    ts(("SK", 0, 144), ("IC", 0, 144), PE, A.is_equal, K12, A.mult)
    act(("SC", 0, 144), ("SK", 0, 144), F.Copy, K12)
    act(("SH", 0, 144), ("SK", 0, 144), F.Copy, 1.0 / (16 * K12))
    ts(("S1", 0, 144), ("SK", 0, 144), 1.0 / K12, A.mult)
    ts(("DZ", 0, M), I15, 0.0, A.is_equal, B25, A.mult)
    act(("NDZ", 0, CW), ("DZ", 0, CW), F.Copy, -1.0)
    ts(("DM", 0, 208), ("I15", 0, 208), PG0, A.is_equal)
    act(("NM", 0, 208), ("DM", 0, 208), F.Copy, -1.0, bias=1.0)
    ts(("DMR", 0, 16), ("IC", 0, 16), PR, A.is_equal)
    act(("DMB", 0, M), ("DM", 0, M))
    op("Y", [(lambda k: lambda: g.sync.dma_start(T.DMB[:, M * k:M * k + M], T.DMB[:, 0:M]))(k) for k in range(1, 16)], [("DMB", 0, M)], [("DMB", M, 2 * NP)],
       1.5, lat=3.0, sem=("ld_mb", 16))
    act(tmp, ("I15", 0, CW), F.Copy, -1.0, bias=16.0)
    tt(("PDC", 0, CW), tmp, ("NDZ", 0, CW), A.add)
    if TWICE:
        tt(("PCC", 0, CW), ("I15", 0, CW), ("DZ", 0, CW), A.add)
    if len(TWICE) < 2:
        act(("CC", 0, CW), ("DZ", 0, CW), F.Copy, 2.0, bias=-16.0)
        act(tmp, ("I15", 0, CW), F.Copy, 2.0)
        tt(("PCD", 0, CW), tmp, ("CC", 0, CW), A.add)
    act(tmp, ("DZ", 0, CW), F.Copy, K12 / B25, bias=4081 * K12)
    tt(("CC", 0, CW), tmp, ("I15", 0, CW), A.add)
    act(("P2H", 0, M), ("IG", 0, M), F.Copy, 256.0)
    ts(("P2L", 0, CW), ("I15", 0, CW), P16, A.add)
    copy(("BC", 0, 6), ("BCi", 0, 6))
    tt(("CIM", 0, M), ("CIM", 0, M), ("DM", 0, M), A.mult)
    fill(("C4K", 0, M), K12)
    fill(("ONE", 0, 128), 1.0)
    fill(("C1", 15, 16), B25)
    fill(("C2", 15, 16), -B25)
    for c in "01":
        fill(("dab" + c, M, MW), 0.0)
    op("V", [lambda: g.vector.tensor_copy(T.thf[:], T.thi[:])], [("thi", 0, 1)], [("thf", 0, 1)], cyc(1))
    op("V", [lambda: g.vector.tensor_scalar(T.G8[:], sl(("IG", 0, 128), 8), sl(PP, 8), None, A.is_equal)], [("IG", 0, 128), PP], [("G8", 0, 128)], cyc(128))
    op("P", [lambda: g.tensor.matmul(T.PK1[:, 504:505], T.G8[:], T.thf[:], True, True)], [("G8", 0, 128), ("thf", 0, 1)], [("PK1", 504, 505)], 0.1)
    copy(("TH", 0, 1), ("PK1", 504, 505))
    bonus[0] = 11
    for c in range(2):
        j, LV, L0T = (CW * c, CW * c + CW), "LV%d" % c, ("L0T%d" % c, 0, 128)
        copy(("LN0%d" % c, 0, CW), ("l0i",) + j)
        copy((LV, 0, CW), ("l0i",) + j)
        mm(("PT%d" % c, 0, 128), [(("zin",) + j, IDB)], p=96)
        copy((LV, CW, MW), ("PT%d" % c, 0, 128), p=96)
        mm(("PT%d" % c, 128, 256), [((LV, 0, CW), R0)], p=96)
        copy(L0T, ("PT%d" % c, 128, 256), p=96)
        for q in range(3):
            b = ("PK%d" % c, "PT%d" % c)[q % 2]
            mm((b, 0, 512), [(L0T, ("SIH", 512 * q, 512 * q + 512), 96)])
            (copy if 3 * c + q in LV0 else act)(("LX0", NP * c + 512 * q, NP * c + 512 * q + 512), (b, 0, 512))

    def spread(k):
        def one(r):
            return lambda: g.affine_select(sl(("LX%d" % k, r, 2 * NP, 16)), sl(("L0R%d" % k, 0, M)), [[0, M]], A.is_ge, 0.0, 0, 0)
        for r in range(16):
            op("G", [one(r)], [("L0R%d" % k, 0, M)], [("LX%d" % k, 0, 2 * NP)], 0.17 + 2 * M * CYC, apart="LX%d" % k)

    def awayabs(out, raw, lv, o):
        for q in range(NP // XW):
            b = bank()
            k = XW * q
            yield q
            for lo in range(0, XW, 512):
                hi = min(XW, lo + 512)
                mm((b, lo, hi), [((lv, CW, MW), ("SIH", k + lo, k + hi), 96), (NIDB, (raw, o + k + lo, o + k + hi))])
            act((out, o + k, o + k + XW), (b, 0, XW), F.Abs)

    def stage1(t, c):
        s, LN = str(c), "LN%d%d" % (t, c)
        j = (CW * c, CW * c + CW)
        PK, LV, MN, KL, ML, RT = "PK" + s, "LV" + s, "MN" + s, "KL" + s, "ML" + s, ("R" if t else "Ri", 0, W)
        if t:
            copy((LV, 0, MW), (LN, 0, MW))
        for q in awayabs("AX" + s, "XG" + s, LV, 0):
            (gath if NP // XW * c + q in XV else sgath)(("XG" + s, XW * q, XW * q + XW), ("X", 0, W), (LN, XW * q // 16, XW * (q + 1) // 16))
        for q in range(BQ):
            k = (NP * q // BQ, NP * (q + 1) // BQ)
            gath(("EQ" + s,) + k, RT, (LN, k[0] // 16, k[1] // 16), ("LX%d" % (t % 4), NP * c + k[0], NP * c + k[1]), A.is_equal)
        dist = [(sel("SK", u), ("AX" + s, 0, NP, u)) for u in range(16)]
        conf = [(sel("SC", u), ("EQ" + s, 0, NP, u)) for u in range(16)]
        PD, PC, NK = (PK, 0, CW), (PK, CW, M), ("NK",) + j
        if c in TWICE and c in CF_:
            mm(PC, [(IDB, ("PCC", 0, CW))] + conf + dist)
            mm(PD, [(IDB, ("PDC", 0, CW))] + dist)
        elif c in TWICE:
            mm(PD, [(IDB, ("PDC", 0, CW))] + dist)
            mm(PC, [(IDB, ("PCC", 0, CW))] + dist + conf)
        else:
            mm(PD, [(IDB, ("PDC", 0, CW))] + dist)
            act(("DS",) + j, PD)
            mm(PC, [(IDB, ("PCD", 0, CW))] + conf)
            tt(PC, PC, ("DS",) + j, A.add)
        tt(NK, PC, ("CC", 0, CW), A.min)
        scan((MN, 0, CW), ("DZ", 0, CW), NK, B25, A.add, A.min)
        tt(("C1", 16, 15 + CW), (MN, 0, CW - 1), ("NK", j[0] + 1, j[1]), A.max)
        scan((MN, CW, M), ("DZ", 0, CW), ("C1", 15, 15 + CW), B25, A.add, A.min)
        ts(("ki" + s, 0, 12), (MN, 15, M, 16), 4095, A.bitwise_and)
        copy((KL, 0, 12), ("ki" + s, 0, 12))
        for x in range(2):
            gath((ML, CW * x, CW * x + CW), ("DM", 0, 16), (KL, 6 * x, 6 * x + 6), (LV, 0, CW), A.mult)
        mm((PK, 384, 396), [(sel("S1", u), (ML, u, M, 16)) for u in range(16)])
        copy((KL, 12, 24), (PK, 384, 396))
        gath(("EDU" + s, 0, M), RT, (KL, 12, 24))
        copy(("EV" + s, 0, M), ("EDU" + s, 0, M))
        mm((PK, 400, 496), [(BOH, (ML, 0, CW))])
        copy(("LR",) + j, (PK, 400, 496))
        gath(("NCB",) + j, RT, (KL, 12, 18), ("NM", j[0] + t, j[1] + t), A.mult)

    def farthest(t, c):
        s, j = str(c), (CW * c, CW * c + CW)
        PK, MT = "PK" + s, "MT" + s
        gath(("KEEP",) + j, ("MN" + s, CW, M), ("BC", 0, 6), ("NK",) + j, A.is_lt)
        tt((PK, 0, CW), (PK, 0, CW), ("KEEP",) + j, A.mult)
        scan((MT, M, M + CW), ("NDZ", 0, CW), (PK, 0, CW), -B25, A.add, A.max)
        tt(("C2", 16, 15 + CW), (MT, M, M + CW - 1), (PK, 1, CW), A.min)
        scan((MT, M + CW, 2 * M), ("NDZ", 0, CW), ("C2", 15, 15 + CW), -B25, A.add, A.max)

    def entries(t, c):
        s = str(c)
        for k in range(2):
            for q in awayabs("AD" + s, "DAB" + s, "LV" + s, NP * k):
                d = (NP * k + XW * q, NP * k + XW * q + XW)
                (gath if NP // XW * (2 * c + k) + q in BYV else sgath)(("DAB" + s,) + d, ("X", 0, W), ("EDU" + s, d[0] // 16, d[1] // 16))
            o = M + CW * k
            mm(("PK" + s, o, o + CW), [(IDB, ("P2H", CW * k, CW * k + CW)), (IDB, ("P2L", 0, CW))]
               + [(sel("SK", u), ("AD" + s, NP * k, NP * k + NP, u)) for u in range(16)])

    def tail(t, c):
        s, j = str(c), (CW * c, CW * c + CW)
        PK, PT, MT, JP, L, dab, Q = "PK" + s, "PT" + s, "MT" + s, "JP" + s, ("LV" + s, 0, CW), "dab" + s, "Q" + s
        scan((MT, 0, M), ("DZ", 0, M), (PK, M, 2 * M), B25, A.add, A.min)
        ts(("kj" + s, 0, 24), (MT, 15, 2 * M, 16), 4095, A.bitwise_and)
        copy((JP, 0, 24), ("kj" + s, 0, 24))
        xa, xb = (dab, 0, CW), (dab, CW, M)
        if c in MX_:
            gath(("DA",) + j, ("DAB" + s, 0, 2 * NP), (JP, 0, 6))
            gath(xa, ("DAB" + s, 0, 2 * NP), (JP, 6, 12), ("DA",) + j, A.max)
            gath(xb, ("DAB" + s, 0, 2 * NP), (JP, 6, 12), ("DA",) + j, A.min)
            mm((PK, CW, M), [(BO, xa), (("NBO", 0, 128), xb)])
        else:
            (sgath if c in SD_ else gath)((dab, 0, M), ("DAB" + s, 0, 2 * NP), (JP, 0, 12))
            mm((PK, CW, M), [(IDB, xa), (NIDB, xb)])
            act(("DA",) + j, (PK, CW, M), F.Abs)
            mm((PK, CW, M), [(BO, ("DA",) + j)])
        ts(("SG",) + j, (PK, CW, M), ("THN", t, t + 1) if t else ("TH", 0, 1), A.is_lt)
        mm((PK, 496, 502), [(sel("SH", u), ("SG", j[0] + u, j[1], 16)) for u in range(16)])
        gath(("ME" + s, 0, M), ("DMB", 0, 2 * NP), (JP, 0, 12), ("EV" + s, 0, M), A.mult)
        (sgath if c in SP_ else gath)(("P12" + s, 0, M), ("DMR", 0, 16), (JP, 12, 24))
        if t < TV - 1:
            mm((PT, 192 + CW, 416), [((dab, 0, 128), HB), ((dab, CW, MW), HB)])
        else:
            mm((PT, 192 + CW, 192 + M), [(HB, xa), (HB, xb)])
        mm((PT, 0, M), [(BOH, ("ME" + s, 0, M)), (NIDH, L, 128, (PT, 0, CW)), (NIDH, L, 128, (PT, CW, M))])
        tt((Q, 0, M), (PT, 0, M), ("P12" + s, 0, M), A.mult)
        Qa, Qb, Eb = (Q, 0, CW), (Q, CW, M), ("EV" + s, CW, M)
        mm((PT, 0, CW), [(HP, Eb), (HN, L), (HN, Qa), (HN, Qb)])
        tt(("EAC" + s, 0, CW), (PT, 0, CW), ("SG",) + j, A.mult)
        mm((PT, 192, 192 + CW), [(IDH, L), (IDH, Qa), (IDH, Qb), (IDH, ("EAC" + s, 0, CW))])
        if t < TV - 1:
            MG = ("MG%d%d" % (t, c), 0, MW)
            ts(MG, (PT, 192, 416), -0.25, A.add)
            send(1, MG, ("LN%d%d" % (t + 1, c), 0, MW), "ar%d%d" % (t + 1, c))
        else:
            ts(("ZU",) + j, (PT, 192 + CW, 192 + M), -0.25, A.add)
            copy(("yzo",) + j, ("ZU",) + j)
            act(("ylo",) + j, (PT, 192, 192 + CW))

    def writes(t):
        mm((PU, 208, 400), [(R0, ("LV0", 0, CW), 128, (PU, 208, 208 + CW))])
        mm((PU, 208, 400), [(R0, ("LV1", 0, CW), 128, (PU, 208 + CW, 400))])
        if t == 0:
            act(("L0R0", 0, M), (PU, 208, 400))
            for k in range(1, N):
                send(k, ("L0R0", 0, M), ("L0R%d" % k, 0, M), "al%d" % k)
        tt(("M2", 0, M), (PU, 208, 400), ("DM", t, t + M), A.mult)

    def update(t):
        mm((PU, 0, M), [(IDH, ("LR", 0, M)), (IDB, ("C4K", 0, M))], last=False)
        pos = 0
        for v in range(12):
            n, c = M - 16 * v, v // 6
            if v % 6 == 0:
                j = (CW * c, CW * c + CW)
                mm((PU,) + j, [(("N4K", 0, 128), ("SG",) + j)], first=False, last=False)
            ts(("EW", pos, pos + n), ("LR", 16 * v, M), ("PK%d" % c, 384 + v % 6, 385 + v % 6), A.is_equal, ("PK%d" % c, 496 + v % 6, 497 + v % 6), A.mult)
            terms = [(("LTR", 0, 128), ("EW", pos, pos + 16), 128, (PU, 16 * v, 16 * v + 16))]
            if v < 11:
                terms.append((("BO4", 0, 128), ("EW", pos + 16, pos + n), 128, (PU, 16 * v + 16, M)))
            mm((PU, 0, M), terms, first=False, last=v == 11)
            pos += n
        tt(("WM", 0, M), (PU, 0, M), ("CIM", 0, M), A.min)
        mm((PU, 192, 204), [(sel("S1", u), ("WM", u, M, 16)) for u in range(16)])
        copy(("WLU", 0, 12), (PU, 192, 204))
        op("V", [lambda: g.vector.tensor_tensor(T.R[:].indirect(sl(("WLU", 0, 12))), sl(("NCB", 0, M)), sl(("M2", 0, M)), A.add)],
           [("WLU", 0, 12), ("NCB", 0, M), ("M2", 0, M)], [("R", 0, RW)], 0.05 + M * 3.5 * CYC)

    def count(t):
        def add(c):
            return lambda: g.scalar.activation(sl(("ACO", 0, 6)), sl(("PK%d" % c, 496, 502)), F.Copy, accum_out=sl(("CNT", c, c + 1)))
        for c in range(2):
            op("S", [add(c)], [("PK%d" % c, 496, 502)], [("ACO", 0, 6), ("CNT", c, c + 1)], 0.13)
        mm((PU, 420, 421), [(("ONE", 0, 128), ("CNT", 0, 1)), (("ONE", 0, 128), ("CNT", 1, 2))], slow=4)
        copy(("ni", 0, 1), (PU, 420, 421))
        ts(("NS%d" % t, 0, 1), ("ni", 0, 1), 63, A.bitwise_and)
        send(1, ("NS%d" % t, 0, 1), ("NL%d" % (t + 1), 0, 1), "an%d" % (t + 1))

    for t in range(TV):
        if t == 0:
            writes(t)
        bonus[0] = 1
        stage1(t, 0)
        bonus[0] = 2
        stage1(t, 1)
        bonus[0] = 3
        if t == 0:
            copy(("R", 0, 1024), ("Ri", 0, 1024))
            copy(("R", 1024, 2048), ("Ri", 1024, 2048))
        else:
            writes(t)
            ts(("THN", t, t + 1), ("NL%d" % t, 0, 1), ("TH", 0, 1), A.add)
        if t < 3:
            spread(t + 1)
        bonus[0] = 4
        farthest(t, 0)
        bonus[0] = 5
        entries(t, 0)
        bonus[0] = 4
        farthest(t, 1)
        bonus[0] = 6
        entries(t, 1)
        bonus[0] = 7
        tail(t, 0)
        bonus[0] = 8
        tail(t, 1)
        bonus[0] = 9
        update(t)
        bonus[0] = 10
        if t < TV - 1:
            count(t)
    bonus[0] = 0
    mm(("XD0", 0, 256), [(("IDF", 0, 128), ("R", 1536, 1792)), (("IDF", 0, 128), ("R", 1792, 2048))], slow=4, last=False)
    for h in range(3):
        copy(("RH", 512 * h, 512 * h + 512), ("R", 512 * h, 512 * h + 512))
        mm(("XD0", 0, 256), [(IDH, ("RH", 512 * h, 512 * h + 256)), (IDH, ("RH", 512 * h + 256, 512 * h + 512))], first=False, last=h == 2)
    act(("yro", 0, 256), ("XD0", 0, 256))
    store(T.yz, ("yzo", 0, M))
    store(T.yl, ("ylo", 0, M))
    store(T.yr, ("yro", 0, 256))
    return build(ops)


def rank_program(g, core, T, topo):
    if T.rank_of(core) is None:
        return
    ops = program(g, core, T, topo)
    order, _ = schedule(ops)
    queue = {"V": g.vector, "S": g.scalar, "P": g.tensor, "G": g, "Y": g.sync}
    own = {"V": "sV", "S": "sS", "P": "sP", "G": "sG"}
    know = {k: {} for k in queue}
    done, last = {}, {}
    for i in order:
        o = ops[i]
        e = o["e"]
        if e == "net":
            s, v = o["sem"]
            done[i], last[s] = (s, v, {s: v}), v
            continue
        kn = know[e]
        for j in sorted(o["d"] - o["free"], key=lambda j: -ops[j]["s"]):
            s, v, clk = done[j]
            if kn.get(s, 0) < v:
                queue[e].wait_ge(T.sem[s], v)
            for a, b in clk.items():
                if kn.get(a, 0) < b:
                    kn[a] = b
        if "send" in o:
            for f in o["f"]:
                f()
            last["snt"] = last.get("snt", 0) + o["send"]
            continue
        s, k = o["sem"] if "sem" in o else (own[e], 1)
        for f in o["f"]:
            f().then_inc(T.sem[s], k)
            last[s] = last.get(s, 0) + k
        clk = dict(kn)
        clk[s] = last[s]
        done[i] = (s, last[s], clk)
    for s, v in last.items():
        if know["G"].get(s, 0) < v:
            g.wait_ge(T.sem[s], v)
